import numpy as np, ml_dtypes
CORES = [16,18,20,22]
N = 4
import mx_ref
BF = ml_dtypes.bfloat16
def cols(t, e):
    v = np.concatenate([t.reshape(128, -1, 4), np.zeros((128, 1, 4), BF)], axis=1)
    return np.ascontiguousarray(v[:, e]).reshape(128, -1)
def cut(t, i, w=512):
    return t[:, w * i:w * i + w]
def f(rng, *shape):
    return mx_ref.flush((rng.standard_normal(shape, dtype=np.float32) * np.exp2(rng.integers(-2, 3, shape[:-1] + (1,)))).astype(BF))
def wide(rng, *shape, cols=0):
    v = rng.standard_normal(shape, dtype=np.float32) * np.exp2(rng.integers(-12, 13, shape)).astype(np.float32)
    if cols: v *= np.repeat(np.exp2(rng.integers(-cols, cols + 1, shape[:-2] + (1, shape[-1] // 4))) * (rng.random(shape[:-2] + (1, shape[-1] // 4)) > 0.0625), 4, axis=-1).astype(np.float32)
    return mx_ref.flush(v.astype(BF))
WD, T, PL, CP, NC = 16, 256, 128, 32, 112
def scores(u, x):
    return np.stack([mx_ref.matmul(mx_ref.quantize(u[r]), mx_ref.quantize(x[r]))[0] for r in range(N)])
def fronts(P):
    a = np.zeros(P.shape, bool)
    v, h = P[1:] != P[:-1], P[:, 1:] != P[:, :-1]
    a[1:] |= v; a[:-1] |= v; a[:, 1:] |= h; a[:, :-1] |= h
    return a
def dealt(P):
    i, j = np.nonzero(fronts(P))
    g = np.full((16 * N + 2, WD + 2), -1)
    g[1:-1, 1:-1] = np.arange(N * T).reshape(16 * N, WD)
    n = np.arange(len(i)); D = np.full((N, PL, 5), -1)
    D[(n // 8) % N, 8 * (n // (8 * N)) + n % 8] = np.stack([g[i + 1, j + 1], g[i, j + 1], g[i + 2, j + 1], g[i + 1, j], g[i + 1, j + 2]], axis=1)
    return D
def needed(P):
    return np.stack([np.bincount(e[e >= 0] // T, minlength=N) for e in [np.unique(k) for k in dealt(P)]])
def broken(P):
    if np.sum(fronts(P)) > PL * N: return ["too many active cells"]
    b = []; D = dealt(P)
    for r in range(N):
        c, e = D[r, :, 0], np.unique(D[r])
        if np.bincount(c[c >= 0] // T, minlength=N).max() > CP: b.append("cells of one stripe dealt to one rank")
        if np.bincount(e[e >= 0] // T, minlength=N).max() > NC: b.append("columns of one stripe that one rank needs")
    return b
def smooth(rng, i):
    a, b = np.indices((16 * N, WD)); g = 0
    for _ in range(6):
        t, k, p = rng.uniform(-1, 1), 0.7 * 0.97 ** i * rng.uniform(0.7, 1.4), rng.uniform(0, 6.2832)
        g = g + np.cos(k * (np.cos(t) * a + np.sin(t) * b) + p)
    return g > 0
def straight(rng, i):
    a = np.indices((16 * N, WD))[0]
    return ((a + rng.integers(1, 4)) // 4) % 2 == 0
def islands(rng, i):
    at = [(0, 0), (15, WD // 2)]
    for c in rng.permutation(N * T):
        if len(at) >= int(N * T * 0.0625 * 0.98 ** i): break
        p, q = divmod(int(c), WD)
        if all(abs(p - a) + abs(q - b) >= 3 for a, b in at): at.append((p, q))
    P = np.zeros((16 * N, WD), bool)
    for p, q in at: P[p, q] = True
    return P
def few(rng, i):
    gone = [int(q) for q in 1 + rng.permutation(N - 1)[:rng.integers(1, 3)]]
    if len(gone) == 2 and abs(gone[0] - gone[1]) == 1: gone.pop()
    here = [q for q in range(N) if q not in gone]
    free = [q for q in here if q - 1 not in gone and q + 1 not in gone]
    P = np.zeros((16 * N, WD), bool)
    for q in here:
        if q - 1 in gone: P[16 * q + 1, rng.integers(0, WD)] = True
        if q + 1 in gone: P[16 * q + 14, rng.integers(0, WD)] = True
    for q in free + here[:rng.integers(0, 2)]: P[16 * q + rng.integers(1, 16 if q + 1 in here else 15), rng.integers(0, WD)] = True
    return P
def heavy(rng, i):
    a, b = np.indices((16 * N, WD)); n = np.zeros(a.shape, int); most = rng.integers(0, N)
    low = b % 2 == 1 if WD == 8 else ((b % 2 == 0) & (b > 0)) | (b == WD - 1)
    for r in range(N):
        if r == most:
            for k in (6, 10): n += a >= 16 * r + k + low
            n += a >= 16 * r + 14
            if WD == 8: n[16 * r + 2, 0] += 1
            else: n += a >= 16 * r + 2
        else:
            w = rng.integers(5, 12) + max(0, 3 - 0.1 * i) * np.sin(rng.uniform(0.2, 0.8) * np.arange(WD) + rng.uniform(0, 6.2832))
            n += a >= 16 * r + np.clip(np.rint(w), 2, 14)[None, :]
    return n % 2 == 0
def borders(rng, i):
    a, b = np.indices((16 * N, WD))
    return (a // 16 + (b < rng.integers(1, WD))) % 2 == 0
def drawn(rng, make, uneven=False, idle=False):
    for i in range(50):
        P = make(rng, i) ^ bool(rng.integers(0, 2))
        c = fronts(P).reshape(N, T).sum(axis=1)
        if c.sum() < (1 if idle else 8 * N) or broken(P): continue
        m = needed(P) * (1 - np.eye(N, dtype=int))
        if uneven and (c.max() < 3 * c.min() or m.max() != NC): continue
        if idle and not 1 <= (c == 0).sum() <= 2: continue
        if idle and (c.sum() > 8 * (N - 1) or (c.sum() - 1) % 8 < 3): continue
        if idle and not (m.sum(axis=0)[c == 0] > 0).all(): continue
        return P
    raise RuntimeError("no field in 50 tries")
def sized(t):
    v = t.astype(np.float32)
    return np.where(np.abs(v) < 2.0 ** -30, np.float32(0), v).astype(BF)
def plant(rng, P, spread=False):
    u = sized(f(rng, 128, 512)); qu = mx_ref.quantize(u)
    x = np.zeros((N, 128, T, 4), BF); want = P.reshape(N, T)
    for r in range(N):
        left = np.arange(T)
        for i in range(50):
            k = len(left); m = 8 * -(-k // 8)
            t = sized(wide(rng, 128, 4 * m, cols=2) if spread else f(rng, 128, 4 * m))
            s = mx_ref.matmul(qu, mx_ref.quantize(t))[0][:k]
            turn = np.where((s > 0) == want[r, left], 1, -1)
            t = (t.astype(np.float32).reshape(128, m, 4)[:, :k] * turn[None, :, None]).astype(BF)
            ok = np.abs(s) > 32
            x[r][:, left[ok]] = t[:, ok]
            left = left[~ok]
            if len(left) == 0: break
        else: raise RuntimeError("scores too small in 50 tries")
    return {"x": x.reshape(N, 128, 4 * T), "u": np.stack([u] * N), "w": sized(f(rng, N, 128, 5120))}
def setup_inputs(rng):
    return plant(rng, drawn(rng, smooth))
def setup_inputs_few(rng):
    return plant(rng, drawn(rng, few, idle=True))
def setup_inputs_near(rng):
    for i in range(50):
        d = plant(rng, drawn(rng, borders))
        s = scores(d["u"], d["x"])
        e = 1 + int(np.floor(np.log2(float(np.abs(s).min()))))
        d["u"] = sized((d["u"].astype(np.float32) * np.float32(2.0 ** -e)).astype(BF))
        t = scores(d["u"], d["x"])
        if 0.5 < np.abs(t).min() <= 1 and np.array_equal(t > 0, s > 0): return d
    raise RuntimeError("no scores near 0.5 in 50 tries")
def setup_inputs_spread(rng):
    return plant(rng, drawn(rng, islands), spread=True)
def setup_inputs_straight(rng):
    return plant(rng, drawn(rng, straight))
def setup_inputs_uneven(rng):
    return plant(rng, drawn(rng, heavy, uneven=True))
def check_inputs(d):
    b = []
    for k in ("x", "u", "w"):
        v = np.abs(d[k].astype(np.float32))
        if not ((v == 0) | ((v >= 2.0 ** -30) & (v <= 2.0 ** 30))).all(): b.append("sizes of " + k)
    if b: return b
    for r in range(N):
        if not np.array_equal(d["u"][r].astype(np.float32), d["u"][0].astype(np.float32)): b.append("u")
    s = scores(d["u"], d["x"])
    if not (np.abs(s) > 0.5).all(): b.append("score")
    return b + broken((s > 0).reshape(16 * N, WD))
def reference(x, u, w):
    P = (scores(u, x) > 0).reshape(16 * N, WD)
    D = dealt(P)
    m = max(8, 8 * -(-int(np.sum(fronts(P))) // (8 * N)))
    X = np.concatenate(list(x), axis=1)
    y = np.zeros((N, 128, 2 * PL), np.float32)
    for r in range(N):
        for k in range(5):
            q = mx_ref.quantize(cols(X, D[r, :m, k]))
            for o in range(2): y[r][:, PL * o:PL * o + m] += mx_ref.matmul(mx_ref.quantize(cut(w[r], 2 * k + o)), q)
    return {"y": y}

@@ -1,0 +1,331 @@
+from concourse.bass import DstId, RemoteDMATransfer
+from concourse.mybir import dt, AluOpType, ActivationFunctionType, AxisListType
+
+A = AluOpType
+F = ActivationFunctionType
+CAP = 144
+CODE = "float8_e4m3fn_x4"
+SCRATCH = {
+    "ut": ("sbuf", [128, 512], "bfloat16"), "xt": ("sbuf", [128, 1024], "bfloat16"),
+    "wt": ("sbuf", [128, 5120], "bfloat16"), "zt": ("sbuf", [128, 640], "bfloat16"),
+    "zb": ("sbuf", [128, 320], "bfloat16"),
+    "uq": ("sbuf", [128, 128], CODE), "us": ("sbuf", [128, 128], "uint8"),
+    "urq": ("sbuf", [128, 128], CODE), "urs": ("sbuf", [128, 128], "uint8"),
+    "winq": ("sbuf", [128, 416], CODE), "wins": ("sbuf", [128, 416], "uint8"),
+    "wq": ("sbuf", [128, 1280], CODE), "ws": ("sbuf", [128, 1280], "uint8"),
+    "eq": ("sbuf", [128, 800], CODE), "es": ("sbuf", [128, 800], "uint8"),
+    "xfq": ("sbuf", [128, 640], CODE), "xfs": ("sbuf", [128, 640], "uint8"),
+    "off0": ("sbuf", [128, 8], "uint16"),
+    "ys": ("sbuf", [128, 256], "float32"),
+    "sc": ("psum", [128, 512], "float32"), "yp": ("psum", [128, 1024], "float32"),
+    "pI": ("sbuf", [128, 1], "int32"), "pm": ("sbuf", [128, 4], "int32"),
+    "p16": ("sbuf", [128, 1], "float32"), "a8": ("sbuf", [128, 1], "float32"), "bc": ("sbuf", [128, 4], "float32"),
+    "corr": ("sbuf", [128, 1], "float32"),
+    "i64": ("sbuf", [128, 8], "float32"), "i16": ("sbuf", [128, 8], "float32"), "y16": ("sbuf", [128, 10], "float32"),
+    "tgt": ("sbuf", [128, 2], "float32"), "nP": ("sbuf", [128, 8], "float32"), "slot": ("sbuf", [128, 8], "float32"),
+    "mth": ("sbuf", [128, 10], "float32"), "mbi": ("sbuf", [128, 10], "float32"),
+    "tt16": ("sbuf", [128, 160], "float32"), "ext1": ("sbuf", [128, 160], "float32"), "ext": ("sbuf", [128, 160], "float32"),
+    "half": ("sbuf", [128, 320], "bfloat16"),
+    "s": ("sbuf", [128, 256], "bfloat16"), "hp": ("sbuf", [128, 288], "bfloat16"), "vp": ("sbuf", [128, 288], "bfloat16"),
+    "m1": ("sbuf", [128, 256], "bfloat16"), "m2": ("sbuf", [128, 256], "bfloat16"), "m3": ("sbuf", [128, 256], "bfloat16"),
+    "l": ("sbuf", [128, 256], "bfloat16"), "pl": ("sbuf", [128, 256], "bfloat16"),
+    "q0": ("sbuf", [128, 16], "bfloat16"), "q15": ("sbuf", [128, 16], "bfloat16"),
+    "inf": ("sbuf", [128, 160], "bfloat16"),
+    "dd": ("sbuf", [128, 48], "float32"), "dq": ("sbuf", [128, 48], "float32"),
+    "e9": ("sbuf", [128, 48], "float32"), "e11": ("sbuf", [128, 48], "float32"),
+    "eb": ("sbuf", [128, 64], "float32"), "et": ("sbuf", [128, 64], "float32"),
+    "xs": ("sbuf", [128, 64], "float32"), "cc": ("sbuf", [128, 4], "float32"), "en": ("sbuf", [128, 4], "float32"),
+    "S": ("sbuf", [128, 256], "bfloat16"),
+    "tI": ("sbuf", [128, 2], "int32"), "tJ": ("sbuf", [128, 2], "int32"), "tb": ("sbuf", [128, 2], "float32"),
+    "nI": ("sbuf", [128, 256], "int32"), "nA": ("sbuf", [128, 256], "int32"), "dm": ("sbuf", [128, 256], "bfloat16"),
+    "d": ("sbuf", [128, 320], "bfloat16"), "f": ("sbuf", [128, 320], "bfloat16"),
+    "b": ("sbuf", [128, 288], "bfloat16"), "tm": ("sbuf", [128, 288], "bfloat16"), "nd": ("sbuf", [128, 288], "bfloat16"),
+    "tab": ("sbuf", [128, 320], "bfloat16"),
+    "junk": ("sbuf", [128, 3200], "bfloat16"), "acl": ("sbuf", [128, 2], "float32"), "acc": ("sbuf", [128, 10], "float32"),
+    "cnt": ("sbuf", [128, 10], "float32"), "ofs": ("sbuf", [128, 10], "uint16"),
+    "cI": ("sbuf", [128, 2], "int32"), "jI": ("sbuf", [128, 2], "int32"),
+    "l3": ("sbuf", [128, 2], "float32"), "l4": ("sbuf", [128, 2], "float32"),
+    "c3": ("sbuf", [128, 2], "float32"), "c4": ("sbuf", [128, 2], "float32"),
+    "iof": ("sbuf", [128, 10], "float32"), "io16": ("sbuf", [128, 10], "uint16"), "ioo": ("sbuf", [128, 10], "uint16"),
+    "g1": ("sbuf", [128, 160], "float32"), "x1": ("sbuf", [128, 160], "float32"),
+    "ix": ("sbuf", [128, 10], "float32"), "ixh": ("sbuf", [128, 5], "float32"), "ixp": ("sbuf", [128, 5], "float32"),
+    "idm": ("sbuf", [128, 8], "uint16"), "li": ("sbuf", [128, 16], "uint16"), "lb": ("sbuf", [128, 16], "uint16"),
+    "lbi": ("sbuf", [128, 16], "int32"), "llo": ("sbuf", [128, 16], "int32"), "lhi": ("sbuf", [128, 16], "int32"),
+    "lo": ("sbuf", [128, 32], "uint16"),
+    "gq": ("sbuf", [128, 32], "float32"), "bq": ("sbuf", [128, 32], "float32"), "fo": ("sbuf", [128, 40], "uint16"),
+}
+for _i in range(3):
+    SCRATCH["of%d" % _i] = ("sbuf", [128, 10], "uint16")
+    SCRATCH["pkq%d" % _i] = ("sbuf", [128, CAP], CODE)
+    SCRATCH["pks%d" % _i] = ("sbuf", [128, CAP], "uint8")
+    SCRATCH["lnq%d" % _i] = ("sbuf", [128, CAP], CODE)
+    SCRATCH["lns%d" % _i] = ("sbuf", [128, CAP], "uint8")
+SEMAPHORES = ["vc", "ac", "tc", "pc", "ldu", "ldx", "ldw0", "ldw1", "ldw2", "zc", "halo", "info", "idx",
+              "cq0", "cq1", "cq2", "cs0", "cs1", "cs2", "sent", "st0", "st1"]
+
+
+def rank_program(g, core, T, topo):
+    r = T.rank_of(core)
+    if r is None:
+        return
+    N = len(T.cores)
+    others = [q for q in range(N) if q != r]
+    Q = {"v": g.vector, "a": g.scalar, "t": g.tensor, "p": g, "s": g.sync}
+    cnt, seen = {}, {}
+
+    def wait(qn, deps):
+        for d in deps:
+            if d is None:
+                continue
+            key = (qn, d[0])
+            if seen.get(key, 0) < d[1]:
+                Q[qn].wait_ge(T.sem[d[0]], d[1])
+                seen[key] = d[1]
+
+    def tok(sem, inst, n):
+        inst.then_inc(T.sem[sem], n)
+        cnt[sem] = cnt.get(sem, 0) + n
+        return (sem, cnt[sem])
+
+    def op(qn, name, deps, *args):
+        wait(qn, deps)
+        q = Q[qn]
+        if name == "memset": i = q.memset(*args)
+        elif name == "tt": i = q.tensor_tensor(*args)
+        elif name == "ts": i = q.tensor_scalar(*args)
+        elif name == "copy": i = q.tensor_copy(*args)
+        elif name == "red": i = q.tensor_reduce(args[0], args[1], AxisListType.X, A.add)
+        elif name == "scan": i = q.tensor_tensor_scan(*args)
+        elif name == "quant": i = q.quantize_mx(*args)
+        elif name == "act": i = q.activation(*args)
+        elif name == "sum": i = q.activation(args[0], args[1], F.Sign, bias=args[2], scale=1.0, accum_out=args[3])
+        elif name == "mm": i = q.matmul_mx(*args)
+        elif name == "iota": i = q.iota(*args)
+        else: i = q.iota(*args, allow_small_or_imprecise_dtypes=True)
+        return tok(qn + "c", i, 1)
+
+    def V(name, deps, *args): return op("v", name, deps, *args)
+    def S(name, deps, *args): return op("a", name, deps, *args)
+
+    def dma(qn, sem, deps, out, in_):
+        wait(qn, deps)
+        return tok(sem, Q[qn].dma_start(out, in_), 16)
+
+    def U8(v): return v.bitcast(dt.uint8)
+    def U32(v): return v.bitcast(dt.uint32)
+
+    ldu = dma("a", "ldu", [], T.ut[:, 0:8], T.u[:, 0:8])
+    ldx = dma("s", "ldx", [], T.xt[:], T.x[:])
+
+    mu = V("memset", [], T.ut[:, 8:512], 0.0)
+    mo = V("memset", [], T.off0[:], 0)
+    mz = V("memset", [], T.zt[:], 0.0)
+    qz = V("quant", [mz], T.winq[:, 288:416], T.wins[:, 288:416], T.zt[:, 0:512])
+    qe = V("quant", [], T.eq[:, 640:800], T.es[:, 640:800], T.zt[:])
+    c = [V("memset", [], T.zb[:], 0.0), V("memset", [], T.half[:], 0.5),
+         V("memset", [], T.hp[:, 0:16], 1.0),
+         V("memset", [], T.vp[:, 0:16], 1.0), V("memset", [], T.vp[:, 256:272], 1.0),
+         V("memset", [], T.d[:, 0:32], 0.0), V("memset", [], T.d[:, 288:320], 0.0),
+         V("memset", [], T.tab[:, 288:320], float(CAP)),
+         V("memset", [], T.eb[:, 48:64], 0.0), V("memset", [], T.et[:, 0:16], 0.0)]
+    k0 = op("p", "iota", [], T.pI[:], [[0, 1]], 0, 1)
+    k1 = op("p", "iotaf", [], T.i64[:], [[64, 8]], 0, 0)
+    k2 = op("p", "iotaf", [], T.i16[:], [[0, 4], [16, 2]], 0, 0)
+    k3 = op("p", "iotaf", [], T.y16[:], [[16, 10]], 0, 0)
+    k4 = op("p", "iotaf", [], T.tt16[:], [[0, 10], [1, 16]], 0, 0)
+    V("ts", [k0], T.pm[:, 0:1], T.pI[:], 15, None, A.bitwise_and)
+    V("ts", [], T.pm[:, 1:2], T.pI[:], 7, None, A.bitwise_and)
+    V("ts", [], T.pm[:, 2:3], T.pI[:], 3, 1, A.logical_shift_right, A.bitwise_and)
+    t = V("ts", [], T.pm[:, 3:4], T.pI[:], 5, None, A.logical_shift_right)
+    V("copy", [t], T.p16[:], T.pm[:, 0:1])
+    V("ts", [], T.a8[:], T.pm[:, 3:4], 8.0, None, A.mult)
+    V("ts", [], T.corr[:], T.pm[:, 0:1], -256.0, 256.0 * 15 + 1, A.mult, A.add)
+    V("ts", [], T.bc[:, 0:1], T.pm[:, 2:3], 32.0, None, A.mult)
+    t = V("copy", [], T.bc[:, 1:2], T.pm[:, 1:2])
+    t = V("tt", [t], T.bc[:, 2:3], T.bc[:, 0:1], T.bc[:, 1:2], A.add)
+    t = V("tt", [t], T.bc[:, 3:4], T.bc[:, 2:3], T.a8[:], A.add)
+    V("ts", [t, k4], T.tgt[:], T.i64[:, 0:2], T.bc[:, 3:4], 1024.0, A.add, A.add)
+    V("ts", [], T.nP[:], T.i64[:], T.bc[:, 2:3], 8.0 * r, A.add, A.add)
+    V("ts", [], T.slot[:], T.i16[:], T.p16[:], None, A.add)
+    t = V("ts", [], T.mth[:], T.y16[:], T.p16[:], None, A.add)
+    V("ts", [t], T.mbi[:], T.mth[:], -1.0, -0.5, A.mult, A.add)
+    t = V("ts", [], T.ext1[:], T.tt16[:], T.p16[:], 512.0, A.is_gt, A.mult)
+    t = V("ts", [t], T.ext[:], T.ext1[:], -256.0, None, A.add)
+    kc = V("memset", [t], T.ext[:, 0:160:16], -5120.0)
+
+    qu = V("quant", [ldu, mu], T.uq[:], T.us[:], T.ut[:])
+    pu = V("copy", [qu, mo], U32(T.urq[:]), U32(T.uq[:]).indirect(T.off0[:]))
+    pv = S("act", [qu, mo], T.urs[:], T.us[:].indirect(T.off0[:]), F.Copy)
+    qx = V("quant", [ldx], T.winq[:, 16:272], T.wins[:, 16:272], T.xt[:])
+    mm = op("t", "mm", [pu, pv, qx], T.sc[:, 0:256], T.urq[:], T.urs[:], T.winq[:, 16:272], T.wins[:, 16:272], True, True)
+
+    halo_in = 0
+    nb = ([(r - 1, 16, 272)] if r > 0 else []) + ([(r + 1, 256, 0)] if r < N - 1 else [])
+    wait("p", [qx])
+    for kind in ("q", "s"):
+        tr = []
+        for k, (q, src, dst) in enumerate(nb):
+            en = topo.engines(core, T.cores[q])
+            w = len(en) // 2
+            rid, pid, _ = topo.addr(T.cores[q])
+            m = sum(1 << e for e in en[k * w:k * w + w])
+            a, b = T["win" + kind][:, src:src + 16], T["win" + kind][:, dst:dst + 16]
+            if kind == "q": a, b = U8(a), U8(b)
+            tr.append(RemoteDMATransfer(dst_ids=[DstId(rid=rid, pnc=pid)], dma_engine_mask=m, remote_sem=T.sem.halo, srcs=[a], dsts=[b]))
+            cnt["sent"] = cnt.get("sent", 0) + w
+            halo_in += w
+        g.remote_dma_fused(tr, local_sem=T.sem.sent)
+    hal = ("halo", halo_in)
+    zc = None
+    if r == 0 or r == N - 1:
+        at = 0 if r == 0 else 272
+        dma("s", "zc", [qz], U8(T.winq[:, at:at + 16]), U8(T.winq[:, 288:304]))
+        zc = dma("s", "zc", [], T.wins[:, at:at + 16], T.wins[:, 288:304])
+
+    s = S("act", [mm], T.s[:], T.sc[:, 0:256], F.Sign)
+    h = V("tt", [s, mm], T.hp[:, 16:271], T.s[:, 0:255], T.sc[:, 1:256], A.mult)
+    v = V("tt", [], T.vp[:, 16:256], T.s[:, 0:240], T.sc[:, 16:256], A.mult)
+    h = V("memset", [h], T.hp[:, 31:272:16], 1.0)
+    v = V("tt", [v, c[4]], T.m2[:], T.vp[:, 16:272], T.vp[:, 0:256], A.min)
+    h = V("tt", [h], T.m1[:], T.hp[:, 16:272], T.hp[:, 15:271], A.min)
+    h = V("tt", [h, v], T.m3[:], T.m1[:], T.m2[:], A.min)
+    l = V("ts", [h], T.l[:], T.m3[:], 0.0, None, A.is_lt)
+    pl = V("scan", [l], T.pl[:], T.l[:], T.zb[:, 0:256], 0.0, A.add, A.add)
+    o = 40 * r
+    V("ts", [], T.q15[:], T.l[:, 240:256], -2.0, 6.0, A.mult, A.add)
+    t = V("ts", [], T.q0[:], T.l[:, 0:16], -1.0, 5.0, A.mult, A.add)
+    V("copy", [pl], T.inf[:, o + 16:o + 18], T.pl[:, 254:256])
+    V("tt", [t], T.inf[:, o + 18:o + 34], T.q15[:], T.s[:, 240:256], A.mult)
+    t = V("tt", [], T.inf[:, o:o + 16], T.q0[:], T.s[:, 0:16], A.mult)
+
+    def span(q): return (40 * q + (16 if q == 0 else 0), 40 * q + (18 if q == N - 1 else 34))
+
+    def to_all(src, dsts, sem):
+        m = topo.mask(core, T.cores[others[0]])
+        ids = []
+        for q in others:
+            rid, pid, _ = topo.addr(T.cores[q])
+            ids.append(DstId(rid=rid, pnc=pid))
+        g.remote_dma_fused([RemoteDMATransfer(dst_ids=ids, dma_engine_mask=m, remote_sem=sem, srcs=[src], dsts=dsts)], local_sem=T.sem.sent)
+        cnt["sent"] += len(topo.engines(core, T.cores[others[0]]))
+    ne = len(topo.engines(core, T.cores[others[0]]))
+    a, b = span(r)
+    wait("p", [t])
+    to_all(T.inf[:, a:b], [T.inf[:, a:b]] * 3, T.sem.info)
+    inf = ("info", 3 * ne)
+    ldw = [dma("s", "ldw%d" % k, [t], T.wt[:, 2048 * k:min(5120, 2048 * k + 2048)], T.w[:, 2048 * k:min(5120, 2048 * k + 2048)]) for k in range(3)]
+
+    for k in range(3):
+        x = V("tt", [inf, t], T.dd[:, 16 * k:16 * k + 16], T.inf[:, 40 * k + 18:40 * k + 34], T.inf[:, 40 * k + 40:40 * k + 56], A.subtract)
+    cc = V("scan", [], T.cc[:], T.inf[:, 17:160:40], T.zb[:, 0:4], 0.0, A.add, A.add)
+    x = V("tt", [x], T.dq[:], T.dd[:], T.dd[:], A.mult)
+    V("ts", [x], T.e9[:], T.dq[:], 81.0, None, A.is_equal)
+    y = V("ts", [], T.e11[:], T.dq[:], 121.0, None, A.is_equal)
+    eb = V("ts", [], T.eb[:, 0:48], T.dq[:], 95.0, None, A.is_ge)
+    et = V("tt", [y], T.et[:, 16:64], T.e9[:], T.e11[:], A.add)
+    xs = V("scan", [et, eb], T.xs[:], T.eb[:], T.et[:], 0.0, A.add, A.add)
+    if r > 0: l = V("tt", [et, t], T.l[:, 0:16], T.l[:, 0:16], T.et[:, 16 * r:16 * r + 16], A.add)
+    if r < N - 1: l = V("tt", [eb, t], T.l[:, 240:256], T.l[:, 240:256], T.eb[:, 16 * r:16 * r + 16], A.add)
+    en = V("tt", [xs, cc], T.en[:], T.xs[:, 15:64:16], T.cc[:], A.add)
+    sS = V("scan", [l], T.S[:], T.l[:], T.zb[:, 0:256], 0.0, A.add, A.add)
+    if r > 0: n = V("ts", [en], T.tI[:], T.tgt[:], T.en[:, r - 1:r], None, A.subtract)
+    else: n = V("copy", [], T.tI[:], T.tgt[:])
+    if r > 0: x = V("ts", [sS], T.nI[:], T.S[:], T.en[:, r - 1:r], -1.0, A.add, A.add)
+    else: x = V("ts", [sS], T.nI[:], T.S[:], -1.0, None, A.add)
+    n = V("ts", [n], T.tJ[:], T.tI[:], 127, None, A.bitwise_and)
+    tb = V("ts", [n], T.tb[:], T.tJ[:], -1.0, -0.5, A.mult, A.add)
+    x = V("ts", [x], T.nA[:], T.nI[:], 24, None, A.bitwise_and)
+    x = V("ts", [x], T.dm[:], T.nA[:], T.a8[:], None, A.is_equal)
+    d = V("tt", [x, l], T.d[:, 32:288], T.dm[:], T.l[:], A.mult)
+    f = V("scan", [d], T.f[:], T.half[:], T.d[:], 0.0, A.mult, A.max)
+    b = V("tt", [], T.b[:], T.d[:, 0:288], T.d[:, 32:320], A.add)
+    x = V("tt", [b, f], T.tm[:], T.b[:], T.f[:, 17:305], A.max)
+    x = V("ts", [x], T.nd[:], T.tm[:], 0.25, None, A.is_ge)
+    tab = V("scan", [x], T.tab[:, 0:288], T.nd[:], T.zb[:, 0:288], 0.0, A.add, A.add)
+    for k in range(2):
+        al = S("sum", [sS, tb], T.junk[:, 288 * k:288 * k + 256], T.S[:], T.tb[:, k:k + 1], T.acl[:, k:k + 1])
+    NA = 6
+    for k in range(NA):
+        ac = S("sum", [tab], T.junk[:, 288 * (k + 2):288 * (k + 3)], T.tab[:, 0:288], T.mbi[:, k:k + 1], T.acc[:, k:k + 1])
+    for k in range(NA, 9):
+        x = V("ts", [tab, kc], T.junk[:, 288 * (k + 2):288 * (k + 3)], T.tab[:, 0:288], T.mth[:, k:k + 1], None, A.is_le)
+    for k in range(NA, 9):
+        x = V("red", [x], T.cnt[:, k:k + 1], T.junk[:, 288 * (k + 2):288 * (k + 3)])
+    V("copy", [x], T.ofs[:, NA:9], T.cnt[:, NA:9])
+    x = V("ts", [ac], T.ofs[:, 0:NA], T.acc[:, 0:NA], -0.5, 144.0, A.mult, A.add)
+    for i, q in enumerate(others):
+        for k in range(4):
+            y = V("copy", [x], T["of%d" % i][32 * k:32 * k + 32, 0:9], T.ofs[32 * q:32 * q + 32, 0:9])
+        pq = V("copy", [y, hal, zc], U32(T["pkq%d" % i][:]), U32(T.winq[:]).indirect(T["of%d" % i][:, 0:9]))
+        ps = S("act", [y, hal, zc], T["pks%d" % i][:], T.wins[:].indirect(T["of%d" % i][:, 0:9]), F.Copy)
+        j = r if r < q else r - 1
+        rid, pid, _ = topo.addr(T.cores[q])
+        m = topo.mask(core, T.cores[q])
+        wait("p", [pq])
+        g.remote_dma(U8(T["lnq%d" % j][:]), U8(T["pkq%d" % i][:]), T.sem["cq%d" % j], T.sem.sent, pid, rid, m)
+        wait("p", [ps])
+        g.remote_dma(T["lns%d" % j][:], T["pks%d" % i][:], T.sem["cs%d" % j], T.sem.sent, pid, rid, m)
+        cnt["sent"] += 2 * ne
+
+    V("ts", [al], T.cI[:], T.acl[:], -0.5, 128.0, A.mult, A.add)
+    V("ts", [], T.iof[:, 0:2], T.acl[:], -0.5, 144.0, A.mult, A.add)
+    V("ts", [], T.iof[:, 2:4], T.acl[:], -0.5, 128.0, A.mult, A.add)
+    V("ts", [], T.iof[:, 4:6], T.acl[:], -0.5, 160.0, A.mult, A.add)
+    V("ts", [], T.l3[:], T.acl[:], -0.5, 143.0, A.mult, A.add)
+    x = V("ts", [], T.l4[:], T.acl[:], -0.5, 145.0, A.mult, A.add)
+    x = V("ts", [x], T.jI[:], T.cI[:], 15, None, A.bitwise_and)
+    V("ts", [x], T.c3[:], T.jI[:], 0.0, 288.0, A.is_equal, A.mult)
+    x = V("ts", [], T.c4[:], T.jI[:], 15.0, 288.0, A.is_equal, A.mult)
+    V("tt", [x], T.iof[:, 6:8], T.l3[:], T.c3[:], A.max)
+    x = V("tt", [], T.iof[:, 8:10], T.l4[:], T.c4[:], A.max)
+    io = V("copy", [x], T.io16[:], T.iof[:])
+    x = V("copy", [io, tab], T.g1[:], T.tab[:].indirect(T.io16[:]))
+    x = V("scan", [x], T.x1[:], T.ext[:], T.g1[:], 0.0, A.add, A.max)
+    x = V("ts", [x], T.ix[:], T.x1[:, 15:160:16], T.corr[:], 0.0, A.subtract, A.max)
+    x = V("ts", [x], T.ixh[:], T.ix[:, 1:10:2], 256.0, None, A.mult)
+    x = V("tt", [x], T.ixp[:], T.ix[:, 0:10:2], T.ixh[:], A.add)
+    x = V("copy", [x], T.idm[:, 0:5], T.ixp[:])
+    wait("p", [x])
+    to_all(T.idm[:, 0:5], [T.li[:, 5 * (r if r < q else r - 1):5 * (r if r < q else r - 1) + 5] for q in others], T.sem.idx)
+    for k in range(4):
+        y = V("copy", [io], T.ioo[32 * k:32 * k + 32, :], T.io16[32 * r:32 * r + 32, :])
+    pe = [V("copy", [y], U32(T.eq[:, 160 * r:160 * r + 160]), U32(T.winq[:]).indirect(T.ioo[:]))]
+    pf = [S("act", [y], T.es[:, 160 * r:160 * r + 160], T.wins[:].indirect(T.ioo[:]), F.Copy)]
+    for k in range(4):
+        x = V("ts", [en], T.gq[:, 8 * k:8 * k + 8], T.nP[:], T.en[:, k:k + 1], 640.0 if k == 3 else 160.0, A.is_ge, A.mult)
+    x = V("tt", [x], T.bq[:, 0:8], T.slot[:], T.gq[:, 0:8], A.add)
+    y = V("tt", [], T.bq[:, 8:16], T.gq[:, 8:16], T.gq[:, 16:24], A.add)
+    x = V("tt", [y], T.bq[:, 16:24], T.bq[:, 0:8], T.bq[:, 8:16], A.add)
+    x = V("tt", [x], T.bq[:, 24:32], T.bq[:, 16:24], T.gq[:, 24:32], A.max)
+    for k in range(5):
+        fo = V("ts", [x], T.fo[:, 8 * k:8 * k + 8], T.bq[:, 24:32], 32.0 * k, None, A.add)
+    for k in range(3):
+        e = min(1280, 512 * k + 512)
+        qw = V("quant", [ldw[k]], T.wq[:, 512 * k:e], T.ws[:, 512 * k:e], T.wt[:, 2048 * k:4 * e])
+
+    ix = ("idx", 3 * ne)
+    for k in range(4):
+        x = V("copy", [ix], T.lb[32 * k:32 * k + 32, 0:15], T.li[32 * r:32 * r + 32, 0:15])
+    x = V("copy", [x], T.lbi[:, 0:15], T.lb[:, 0:15])
+    V("ts", [x], T.llo[:, 0:15], T.lbi[:, 0:15], 255, None, A.bitwise_and)
+    x = V("ts", [], T.lhi[:, 0:15], T.lbi[:, 0:15], 8, None, A.logical_shift_right)
+    V("copy", [x], T.lo[:, 0:30:2], T.llo[:, 0:15])
+    x = V("copy", [], T.lo[:, 1:30:2], T.lhi[:, 0:15])
+    for i, q in enumerate(others):
+        pe.append(V("copy", [x, ("cq%d" % i, ne)], U32(T.eq[:, 160 * q:160 * q + 160]), U32(T["lnq%d" % i][:]).indirect(T.lo[:, 10 * i:10 * i + 10])))
+        pf.append(S("act", [x, ("cs%d" % i, ne)], T.es[:, 160 * q:160 * q + 160], T["lns%d" % i][:].indirect(T.lo[:, 10 * i:10 * i + 10]), F.Copy))
+    for k in range(5):
+        lo, hi = 128 * k, 128 * k + 128
+        a = V("copy", [pe[-1], fo], U32(T.xfq[:, lo:hi]), U32(T.eq[:]).indirect(T.fo[:, 8 * k:8 * k + 8]))
+        b = S("act", [pf[-1], fo], T.xfs[:, lo:hi], T.es[:].indirect(T.fo[:, 8 * k:8 * k + 8]), F.Copy)
+        ms = []
+        for o in range(2):
+            w = 128 * (2 * k + o)
+            ms.append(op("t", "mm", [a, b, qw], T.yp[:, 512 * o:512 * o + 128], T.wq[:, w:w + 128], T.ws[:, w:w + 128],
+                         T.xfq[:, lo:hi], T.xfs[:, lo:hi], k == 0, k == 4))
+    x = V("copy", [ms[0]], T.ys[:, 0:128], T.yp[:, 0:128])
+    s0 = dma("s", "st0", [x], T.y[:, 0:128], T.ys[:, 0:128])
+    x = S("act", [ms[1]], T.ys[:, 128:256], T.yp[:, 512:640], F.Copy)
+    s1 = dma("a", "st1", [x], T.y[:, 128:256], T.ys[:, 128:256])
+    wait("p", [(k, n) for k, n in cnt.items()])
+    wait("p", [hal, inf, ix])

@@ -4,62 +4,42 @@ from concourse.mybir import dt, AluOpType, ActivationFunctionType, AxisListType
 A = AluOpType
 F = ActivationFunctionType
 CAP = 144
+NA = 7
 CODE = "float8_e4m3fn_x4"
+
+
+def sb(n, d="float32"): return ("sbuf", [128, n], d)
+
+
+BF, I32, U16 = "bfloat16", "int32", "uint16"
 SCRATCH = {
-    "ut": ("sbuf", [128, 512], "bfloat16"), "xt": ("sbuf", [128, 1024], "bfloat16"),
-    "wt": ("sbuf", [128, 5120], "bfloat16"), "zt": ("sbuf", [128, 640], "bfloat16"),
-    "zb": ("sbuf", [128, 320], "bfloat16"),
-    "uq": ("sbuf", [128, 128], CODE), "us": ("sbuf", [128, 128], "uint8"),
-    "urq": ("sbuf", [128, 128], CODE), "urs": ("sbuf", [128, 128], "uint8"),
-    "winq": ("sbuf", [128, 416], CODE), "wins": ("sbuf", [128, 416], "uint8"),
-    "wq": ("sbuf", [128, 1280], CODE), "ws": ("sbuf", [128, 1280], "uint8"),
-    "eq": ("sbuf", [128, 800], CODE), "es": ("sbuf", [128, 800], "uint8"),
-    "xfq": ("sbuf", [128, 640], CODE), "xfs": ("sbuf", [128, 640], "uint8"),
-    "off0": ("sbuf", [128, 8], "uint16"),
-    "ys": ("sbuf", [128, 256], "float32"),
+    "ut": sb(512, BF), "xt": sb(1024, BF), "wt": sb(5120, BF), "zt": sb(640, BF), "zb": sb(320, BF),
+    "uq": sb(128, CODE), "us": sb(128, "uint8"), "urq": sb(128, CODE), "urs": sb(128, "uint8"),
+    "winq": sb(416, CODE), "wins": sb(416, "uint8"),
+    "wq": sb(1280, CODE), "ws": sb(1280, "uint8"),
+    "eq": sb(800, CODE), "es": sb(800, "uint8"),
+    "xfq": sb(640, CODE), "xfs": sb(640, "uint8"),
+    "off0": sb(8, U16), "ys": sb(256),
     "sc": ("psum", [128, 512], "float32"), "yp": ("psum", [128, 1024], "float32"),
-    "pI": ("sbuf", [128, 1], "int32"), "pm": ("sbuf", [128, 4], "int32"),
-    "p16": ("sbuf", [128, 1], "float32"), "a8": ("sbuf", [128, 1], "float32"), "bc": ("sbuf", [128, 4], "float32"),
-    "corr": ("sbuf", [128, 1], "float32"),
-    "i64": ("sbuf", [128, 8], "float32"), "i16": ("sbuf", [128, 8], "float32"), "y16": ("sbuf", [128, 10], "float32"),
-    "tgt": ("sbuf", [128, 2], "float32"), "nP": ("sbuf", [128, 8], "float32"), "slot": ("sbuf", [128, 8], "float32"),
-    "mth": ("sbuf", [128, 10], "float32"), "mbi": ("sbuf", [128, 10], "float32"),
-    "tt16": ("sbuf", [128, 160], "float32"), "ext1": ("sbuf", [128, 160], "float32"), "ext": ("sbuf", [128, 160], "float32"),
-    "half": ("sbuf", [128, 320], "bfloat16"),
-    "s": ("sbuf", [128, 256], "bfloat16"), "hp": ("sbuf", [128, 288], "bfloat16"), "vp": ("sbuf", [128, 288], "bfloat16"),
-    "m1": ("sbuf", [128, 256], "bfloat16"), "m2": ("sbuf", [128, 256], "bfloat16"), "m3": ("sbuf", [128, 256], "bfloat16"),
-    "l": ("sbuf", [128, 256], "bfloat16"), "pl": ("sbuf", [128, 256], "bfloat16"),
-    "q0": ("sbuf", [128, 16], "bfloat16"), "q15": ("sbuf", [128, 16], "bfloat16"),
-    "inf": ("sbuf", [128, 160], "bfloat16"),
-    "dd": ("sbuf", [128, 48], "float32"), "dq": ("sbuf", [128, 48], "float32"),
-    "e9": ("sbuf", [128, 48], "float32"), "e11": ("sbuf", [128, 48], "float32"),
-    "eb": ("sbuf", [128, 64], "float32"), "et": ("sbuf", [128, 64], "float32"),
-    "xs": ("sbuf", [128, 64], "float32"), "cc": ("sbuf", [128, 4], "float32"), "en": ("sbuf", [128, 4], "float32"),
-    "S": ("sbuf", [128, 256], "bfloat16"),
-    "tI": ("sbuf", [128, 2], "int32"), "tJ": ("sbuf", [128, 2], "int32"), "tb": ("sbuf", [128, 2], "float32"),
-    "nI": ("sbuf", [128, 256], "int32"), "nA": ("sbuf", [128, 256], "int32"), "dm": ("sbuf", [128, 256], "bfloat16"),
-    "d": ("sbuf", [128, 320], "bfloat16"), "f": ("sbuf", [128, 320], "bfloat16"),
-    "b": ("sbuf", [128, 288], "bfloat16"), "tm": ("sbuf", [128, 288], "bfloat16"), "nd": ("sbuf", [128, 288], "bfloat16"),
-    "tab": ("sbuf", [128, 320], "bfloat16"),
-    "junk": ("sbuf", [128, 3200], "bfloat16"), "acl": ("sbuf", [128, 2], "float32"), "acc": ("sbuf", [128, 10], "float32"),
-    "cnt": ("sbuf", [128, 10], "float32"), "ofs": ("sbuf", [128, 10], "uint16"),
-    "cI": ("sbuf", [128, 2], "int32"), "jI": ("sbuf", [128, 2], "int32"),
-    "l3": ("sbuf", [128, 2], "float32"), "l4": ("sbuf", [128, 2], "float32"),
-    "c3": ("sbuf", [128, 2], "float32"), "c4": ("sbuf", [128, 2], "float32"),
-    "iof": ("sbuf", [128, 10], "float32"), "io16": ("sbuf", [128, 10], "uint16"), "ioo": ("sbuf", [128, 10], "uint16"),
-    "g1": ("sbuf", [128, 160], "float32"), "x1": ("sbuf", [128, 160], "float32"),
-    "ix": ("sbuf", [128, 10], "float32"), "ixh": ("sbuf", [128, 5], "float32"), "ixp": ("sbuf", [128, 5], "float32"),
-    "idm": ("sbuf", [128, 8], "uint16"), "li": ("sbuf", [128, 16], "uint16"), "lb": ("sbuf", [128, 16], "uint16"),
-    "lbi": ("sbuf", [128, 16], "int32"), "llo": ("sbuf", [128, 16], "int32"), "lhi": ("sbuf", [128, 16], "int32"),
-    "lo": ("sbuf", [128, 32], "uint16"),
-    "gq": ("sbuf", [128, 32], "float32"), "bq": ("sbuf", [128, 32], "float32"), "fo": ("sbuf", [128, 40], "uint16"),
+    "pI": sb(1, I32), "pm": sb(4, I32), "p16": sb(1), "a8": sb(1), "bc": sb(4), "corr": sb(1),
+    "i64": sb(8), "i16": sb(8), "y16": sb(10), "tgt": sb(2), "nP": sb(8), "slot": sb(8), "mth": sb(10), "mbi": sb(10),
+    "tt16": sb(160), "ext1": sb(160), "ext": sb(160), "half": sb(320, BF),
+    "s": sb(256, BF), "hp": sb(288, BF), "vp": sb(288, BF), "m1": sb(256, BF), "m2": sb(256, BF), "m3": sb(256, BF), "gh": sb(256, BF),
+    "l": sb(256, BF), "pl": sb(256, BF), "q0": sb(16, BF), "q15": sb(16, BF), "inf": sb(160, BF),
+    "dd": sb(48), "dq": sb(48), "e9": sb(48), "e11": sb(48), "eb": sb(64), "et": sb(64), "xs": sb(64), "cc": sb(4), "en": sb(4),
+    "S": sb(256, BF), "tI": sb(2, I32), "tJ": sb(2, I32), "tb": sb(2), "nI": sb(256, I32), "nA": sb(256, I32), "dm": sb(256, BF),
+    "d": sb(320, BF), "f": sb(320, BF), "b": sb(288, BF), "tm": sb(288, BF), "nd": sb(288, BF), "tab": sb(320, BF),
+    "junk": sb(3200, BF), "acl": sb(2), "acc": sb(10), "cnt": sb(10), "ofs": sb(10, U16),
+    "cI": sb(2, I32), "jI": sb(2, I32), "l3": sb(2), "l4": sb(2), "c3": sb(2), "c4": sb(2),
+    "iof": sb(10), "io16": sb(10, U16), "ioo": sb(10, U16), "g1": sb(160), "x1": sb(160), "ix": sb(10), "ixh": sb(5), "ixp": sb(5),
+    "idm": sb(8, U16), "li": sb(16, U16), "lb": sb(16, U16), "lbi": sb(16, I32), "llo": sb(16, I32), "lhi": sb(16, I32), "lo": sb(32, U16),
+    "gq": sb(32), "bq": sb(32), "fo": sb(40, U16),
 }
 for _i in range(3):
-    SCRATCH["of%d" % _i] = ("sbuf", [128, 10], "uint16")
-    SCRATCH["pkq%d" % _i] = ("sbuf", [128, CAP], CODE)
-    SCRATCH["pks%d" % _i] = ("sbuf", [128, CAP], "uint8")
-    SCRATCH["lnq%d" % _i] = ("sbuf", [128, CAP], CODE)
-    SCRATCH["lns%d" % _i] = ("sbuf", [128, CAP], "uint8")
+    SCRATCH["of%d" % _i] = sb(10, U16)
+    for _n in ("pk", "ln"):
+        SCRATCH["%sq%d" % (_n, _i)] = sb(CAP, CODE)
+        SCRATCH["%ss%d" % (_n, _i)] = sb(CAP, "uint8")
 SEMAPHORES = ["vc", "ac", "tc", "pc", "ldu", "ldx", "ldw0", "ldw1", "ldw2", "zc", "halo", "info", "idx",
               "cq0", "cq1", "cq2", "cs0", "cs1", "cs2", "sent", "st0", "st1"]
 
@@ -71,16 +51,13 @@ def rank_program(g, core, T, topo):
     N = len(T.cores)
     others = [q for q in range(N) if q != r]
     Q = {"v": g.vector, "a": g.scalar, "t": g.tensor, "p": g, "s": g.sync}
-    cnt, seen = {}, {}
+    cnt, seen = {"sent": 0}, {}
 
     def wait(qn, deps):
         for d in deps:
-            if d is None:
-                continue
-            key = (qn, d[0])
-            if seen.get(key, 0) < d[1]:
+            if d is not None and seen.get((qn, d[0]), 0) < d[1]:
                 Q[qn].wait_ge(T.sem[d[0]], d[1])
-                seen[key] = d[1]
+                seen[(qn, d[0])] = d[1]
 
     def tok(sem, inst, n):
         inst.then_inc(T.sem[sem], n)
@@ -113,45 +90,40 @@ def rank_program(g, core, T, topo):
 
     def U8(v): return v.bitcast(dt.uint8)
     def U32(v): return v.bitcast(dt.uint32)
+    def bits(en): return sum(1 << e for e in en)
+
+    def dest(q):
+        rid, pid, _ = topo.addr(T.cores[q])
+        return DstId(rid=rid, pnc=pid)
+
+    def send(trs):
+        g.remote_dma_fused([RemoteDMATransfer(dst_ids=[dest(q) for q in qs], dma_engine_mask=bits(en), remote_sem=sem, srcs=[src], dsts=dsts)
+                            for qs, en, sem, src, dsts in trs], local_sem=T.sem.sent)
+        cnt["sent"] += sum(len(t[1]) for t in trs)
+
+    def at(q, me): return q if q < me else q - 1
+    eng = {q: topo.engines(core, T.cores[q]) for q in others}
+    ne = min(len(eng[q]) for q in others)
+    W = lambda k: slice(512 * k, min(1280, 512 * k + 512))
+    W4 = lambda k: slice(2048 * k, min(5120, 2048 * k + 2048))
 
     ldu = dma("a", "ldu", [], T.ut[:, 0:8], T.u[:, 0:8])
     ldx = dma("s", "ldx", [], T.xt[:], T.x[:])
-
     mu = V("memset", [], T.ut[:, 8:512], 0.0)
     mo = V("memset", [], T.off0[:], 0)
+    V("memset", [], T.hp[:, 0:16], 1.0)
+    V("memset", [], T.vp[:, 0:16], 1.0)
+    cv = V("memset", [], T.vp[:, 256:272], 1.0)
+    V("memset", [], T.zb[:], 0.0)
     mz = V("memset", [], T.zt[:], 0.0)
+    ch = V("memset", [], T.half[:], 0.5)
     qz = V("quant", [mz], T.winq[:, 288:416], T.wins[:, 288:416], T.zt[:, 0:512])
-    qe = V("quant", [], T.eq[:, 640:800], T.es[:, 640:800], T.zt[:])
-    c = [V("memset", [], T.zb[:], 0.0), V("memset", [], T.half[:], 0.5),
-         V("memset", [], T.hp[:, 0:16], 1.0),
-         V("memset", [], T.vp[:, 0:16], 1.0), V("memset", [], T.vp[:, 256:272], 1.0),
-         V("memset", [], T.d[:, 0:32], 0.0), V("memset", [], T.d[:, 288:320], 0.0),
-         V("memset", [], T.tab[:, 288:320], float(CAP)),
-         V("memset", [], T.eb[:, 48:64], 0.0), V("memset", [], T.et[:, 0:16], 0.0)]
     k0 = op("p", "iota", [], T.pI[:], [[0, 1]], 0, 1)
-    k1 = op("p", "iotaf", [], T.i64[:], [[64, 8]], 0, 0)
-    k2 = op("p", "iotaf", [], T.i16[:], [[0, 4], [16, 2]], 0, 0)
-    k3 = op("p", "iotaf", [], T.y16[:], [[16, 10]], 0, 0)
+    op("p", "iotaf", [], T.i64[:], [[64, 8]], 0, 0)
+    op("p", "iotaf", [], T.i16[:], [[0, 4], [16, 2]], 0, 0)
+    op("p", "iotaf", [], T.y16[:], [[16, 10]], 0, 0)
     k4 = op("p", "iotaf", [], T.tt16[:], [[0, 10], [1, 16]], 0, 0)
-    V("ts", [k0], T.pm[:, 0:1], T.pI[:], 15, None, A.bitwise_and)
-    V("ts", [], T.pm[:, 1:2], T.pI[:], 7, None, A.bitwise_and)
-    V("ts", [], T.pm[:, 2:3], T.pI[:], 3, 1, A.logical_shift_right, A.bitwise_and)
-    t = V("ts", [], T.pm[:, 3:4], T.pI[:], 5, None, A.logical_shift_right)
-    V("copy", [t], T.p16[:], T.pm[:, 0:1])
-    V("ts", [], T.a8[:], T.pm[:, 3:4], 8.0, None, A.mult)
-    V("ts", [], T.corr[:], T.pm[:, 0:1], -256.0, 256.0 * 15 + 1, A.mult, A.add)
-    V("ts", [], T.bc[:, 0:1], T.pm[:, 2:3], 32.0, None, A.mult)
-    t = V("copy", [], T.bc[:, 1:2], T.pm[:, 1:2])
-    t = V("tt", [t], T.bc[:, 2:3], T.bc[:, 0:1], T.bc[:, 1:2], A.add)
-    t = V("tt", [t], T.bc[:, 3:4], T.bc[:, 2:3], T.a8[:], A.add)
-    V("ts", [t, k4], T.tgt[:], T.i64[:, 0:2], T.bc[:, 3:4], 1024.0, A.add, A.add)
-    V("ts", [], T.nP[:], T.i64[:], T.bc[:, 2:3], 8.0 * r, A.add, A.add)
-    V("ts", [], T.slot[:], T.i16[:], T.p16[:], None, A.add)
-    t = V("ts", [], T.mth[:], T.y16[:], T.p16[:], None, A.add)
-    V("ts", [t], T.mbi[:], T.mth[:], -1.0, -0.5, A.mult, A.add)
-    t = V("ts", [], T.ext1[:], T.tt16[:], T.p16[:], 512.0, A.is_gt, A.mult)
-    t = V("ts", [t], T.ext[:], T.ext1[:], -256.0, None, A.add)
-    kc = V("memset", [t], T.ext[:, 0:160:16], -5120.0)
+    ldw = [dma("s", "ldw0", [ldx], T.wt[:, W4(0)], T.w[:, W4(0)])]
 
     qu = V("quant", [ldu, mu], T.uq[:], T.us[:], T.ut[:])
     pu = V("copy", [qu, mo], U32(T.urq[:]), U32(T.uq[:]).indirect(T.off0[:]))
@@ -159,37 +131,28 @@ def rank_program(g, core, T, topo):
     qx = V("quant", [ldx], T.winq[:, 16:272], T.wins[:, 16:272], T.xt[:])
     mm = op("t", "mm", [pu, pv, qx], T.sc[:, 0:256], T.urq[:], T.urs[:], T.winq[:, 16:272], T.wins[:, 16:272], True, True)
 
-    halo_in = 0
     nb = ([(r - 1, 16, 272)] if r > 0 else []) + ([(r + 1, 256, 0)] if r < N - 1 else [])
+
+    def strips(view):
+        send([([q], eng[q][k * (ne // 2):(k + 1) * (ne // 2)], T.sem.halo, view(src, src + 16), [view(dst, dst + 16)])
+              for k, (q, src, dst) in enumerate(nb)])
     wait("p", [qx])
-    for kind in ("q", "s"):
-        tr = []
-        for k, (q, src, dst) in enumerate(nb):
-            en = topo.engines(core, T.cores[q])
-            w = len(en) // 2
-            rid, pid, _ = topo.addr(T.cores[q])
-            m = sum(1 << e for e in en[k * w:k * w + w])
-            a, b = T["win" + kind][:, src:src + 16], T["win" + kind][:, dst:dst + 16]
-            if kind == "q": a, b = U8(a), U8(b)
-            tr.append(RemoteDMATransfer(dst_ids=[DstId(rid=rid, pnc=pid)], dma_engine_mask=m, remote_sem=T.sem.halo, srcs=[a], dsts=[b]))
-            cnt["sent"] = cnt.get("sent", 0) + w
-            halo_in += w
-        g.remote_dma_fused(tr, local_sem=T.sem.sent)
-    hal = ("halo", halo_in)
-    zc = None
-    if r == 0 or r == N - 1:
-        at = 0 if r == 0 else 272
-        dma("s", "zc", [qz], U8(T.winq[:, at:at + 16]), U8(T.winq[:, 288:304]))
-        zc = dma("s", "zc", [], T.wins[:, at:at + 16], T.wins[:, 288:304])
+    strips(lambda a, b: U8(T.winq[:, a:b]))
+    hal, zc = ("halo", 2 * len(nb) * (ne // 2)), None
+    if len(nb) == 1:
+        to = 0 if r == 0 else 272
+        dma("s", "zc", [qz], U8(T.winq[:, to:to + 16]), U8(T.winq[:, 288:304]))
+        zc = dma("s", "zc", [], T.wins[:, to:to + 16], T.wins[:, 288:304])
 
     s = S("act", [mm], T.s[:], T.sc[:, 0:256], F.Sign)
     h = V("tt", [s, mm], T.hp[:, 16:271], T.s[:, 0:255], T.sc[:, 1:256], A.mult)
     v = V("tt", [], T.vp[:, 16:256], T.s[:, 0:240], T.sc[:, 16:256], A.mult)
     h = V("memset", [h], T.hp[:, 31:272:16], 1.0)
-    v = V("tt", [v, c[4]], T.m2[:], T.vp[:, 16:272], T.vp[:, 0:256], A.min)
-    h = V("tt", [h], T.m1[:], T.hp[:, 16:272], T.hp[:, 15:271], A.min)
-    h = V("tt", [h, v], T.m3[:], T.m1[:], T.m2[:], A.min)
-    l = V("ts", [h], T.l[:], T.m3[:], 0.0, None, A.is_lt)
+    v = V("tt", [v, cv], T.m2[:], T.vp[:, 16:272], T.vp[:, 0:256], A.min)
+    h = V("ts", [h], T.m1[:], T.hp[:, 16:272], 0.0, -1.0, A.is_lt, A.mult)
+    h = V("scan", [h, ch], T.gh[:], T.half[:, 0:256], T.m1[:], 0.0, A.mult, A.min)
+    h = V("tt", [h, v], T.m3[:], T.gh[:], T.m2[:], A.min)
+    l = V("ts", [h], T.l[:], T.m3[:], -0.375, None, A.is_le)
     pl = V("scan", [l], T.pl[:], T.l[:], T.zb[:, 0:256], 0.0, A.add, A.add)
     o = 40 * r
     V("ts", [], T.q15[:], T.l[:, 240:256], -2.0, 6.0, A.mult, A.add)
@@ -197,135 +160,167 @@ def rank_program(g, core, T, topo):
     V("copy", [pl], T.inf[:, o + 16:o + 18], T.pl[:, 254:256])
     V("tt", [t], T.inf[:, o + 18:o + 34], T.q15[:], T.s[:, 240:256], A.mult)
     t = V("tt", [], T.inf[:, o:o + 16], T.q0[:], T.s[:, 0:16], A.mult)
-
-    def span(q): return (40 * q + (16 if q == 0 else 0), 40 * q + (18 if q == N - 1 else 34))
-
-    def to_all(src, dsts, sem):
-        m = topo.mask(core, T.cores[others[0]])
-        ids = []
-        for q in others:
-            rid, pid, _ = topo.addr(T.cores[q])
-            ids.append(DstId(rid=rid, pnc=pid))
-        g.remote_dma_fused([RemoteDMATransfer(dst_ids=ids, dma_engine_mask=m, remote_sem=sem, srcs=[src], dsts=dsts)], local_sem=T.sem.sent)
-        cnt["sent"] += len(topo.engines(core, T.cores[others[0]]))
-    ne = len(topo.engines(core, T.cores[others[0]]))
-    a, b = span(r)
+    a, b = o + (16 if r == 0 else 0), o + (18 if r == N - 1 else 34)
     wait("p", [t])
-    to_all(T.inf[:, a:b], [T.inf[:, a:b]] * 3, T.sem.info)
+    send([(others, eng[others[0]], T.sem.info, T.inf[:, a:b], [T.inf[:, a:b]] * 3)])
     inf = ("info", 3 * ne)
-    ldw = [dma("s", "ldw%d" % k, [t], T.wt[:, 2048 * k:min(5120, 2048 * k + 2048)], T.w[:, 2048 * k:min(5120, 2048 * k + 2048)]) for k in range(3)]
+    strips(lambda a, b: T.wins[:, a:b])
+    ldw += [dma("s", "ldw%d" % k, [t], T.wt[:, W4(k)], T.w[:, W4(k)]) for k in (1, 2)]
+
+    V("ts", [k0], T.pm[:, 0:1], T.pI[:], 15, None, A.bitwise_and)
+    V("ts", [], T.pm[:, 1:2], T.pI[:], 7, None, A.bitwise_and)
+    V("ts", [], T.pm[:, 2:3], T.pI[:], 3, 1, A.logical_shift_right, A.bitwise_and)
+    k = V("ts", [], T.pm[:, 3:4], T.pI[:], 5, None, A.logical_shift_right)
+    V("memset", [], T.d[:, 0:32], 0.0)
+    V("copy", [k], T.p16[:], T.pm[:, 0:1])
+    V("ts", [], T.a8[:], T.pm[:, 3:4], 8.0, None, A.mult)
+    V("ts", [], T.corr[:], T.pm[:, 0:1], -256.0, 256.0 * 15 + 1, A.mult, A.add)
+    V("ts", [], T.bc[:, 0:1], T.pm[:, 2:3], 32.0, None, A.mult)
+    k = V("copy", [], T.bc[:, 1:2], T.pm[:, 1:2])
+    V("memset", [], T.d[:, 288:320], 0.0)
+    k1 = V("ts", [k4, k], T.mth[:], T.y16[:], T.p16[:], None, A.add)
+    k = V("tt", [k], T.bc[:, 2:3], T.bc[:, 0:1], T.bc[:, 1:2], A.add)
+    V("memset", [], T.tab[:, 288:320], float(CAP))
+    V("ts", [k1], T.mbi[:], T.mth[:], -1.0, -0.5, A.mult, A.add)
+    k = V("tt", [k], T.bc[:, 3:4], T.bc[:, 2:3], T.a8[:], A.add)
+    k1 = V("ts", [], T.ext1[:], T.tt16[:], T.p16[:], 512.0, A.is_gt, A.mult)
+    V("memset", [], T.eb[:, 48:64], 0.0)
+    V("memset", [], T.et[:, 0:16], 0.0)
+    V("ts", [k], T.tgt[:], T.i64[:, 0:2], T.bc[:, 3:4], 1023.0, A.add, A.add)
+    k1 = V("ts", [k1], T.ext[:], T.ext1[:], -256.0, None, A.add)
+    V("ts", [], T.nP[:], T.i64[:], T.bc[:, 2:3], 8.0 * r, A.add, A.add)
+    V("ts", [], T.slot[:], T.i16[:], T.p16[:], None, A.add)
+    kc = V("memset", [k1], T.ext[:, 0:160:16], -5120.0)
+    V("quant", [], T.eq[:, 640:800], T.es[:, 640:800], T.zt[:])
+    V("quant", [ldw[0]], T.wq[:, W(0)], T.ws[:, W(0)], T.wt[:, W4(0)])
 
     for k in range(3):
-        x = V("tt", [inf, t], T.dd[:, 16 * k:16 * k + 16], T.inf[:, 40 * k + 18:40 * k + 34], T.inf[:, 40 * k + 40:40 * k + 56], A.subtract)
-    cc = V("scan", [], T.cc[:], T.inf[:, 17:160:40], T.zb[:, 0:4], 0.0, A.add, A.add)
+        x = V("tt", [inf, t, kc], T.dd[:, 16 * k:16 * k + 16], T.inf[:, 40 * k + 18:40 * k + 34], T.inf[:, 40 * k + 40:40 * k + 56], A.subtract)
+    cc = V("scan", [], T.cc[:], T.inf[:, 17:160:40], T.zb[:, 0:4], -1.0, A.add, A.add)
     x = V("tt", [x], T.dq[:], T.dd[:], T.dd[:], A.mult)
     V("ts", [x], T.e9[:], T.dq[:], 81.0, None, A.is_equal)
     y = V("ts", [], T.e11[:], T.dq[:], 121.0, None, A.is_equal)
     eb = V("ts", [], T.eb[:, 0:48], T.dq[:], 95.0, None, A.is_ge)
     et = V("tt", [y], T.et[:, 16:64], T.e9[:], T.e11[:], A.add)
-    xs = V("scan", [et, eb], T.xs[:], T.eb[:], T.et[:], 0.0, A.add, A.add)
-    if r > 0: l = V("tt", [et, t], T.l[:, 0:16], T.l[:, 0:16], T.et[:, 16 * r:16 * r + 16], A.add)
     if r < N - 1: l = V("tt", [eb, t], T.l[:, 240:256], T.l[:, 240:256], T.eb[:, 16 * r:16 * r + 16], A.add)
-    en = V("tt", [xs, cc], T.en[:], T.xs[:, 15:64:16], T.cc[:], A.add)
+    if r > 0: l = V("tt", [et, t], T.l[:, 0:16], T.l[:, 0:16], T.et[:, 16 * r:16 * r + 16], A.add)
+    xs = V("scan", [et], T.xs[:], T.eb[:], T.et[:], 0.0, A.add, A.add)
     sS = V("scan", [l], T.S[:], T.l[:], T.zb[:, 0:256], 0.0, A.add, A.add)
-    if r > 0: n = V("ts", [en], T.tI[:], T.tgt[:], T.en[:, r - 1:r], None, A.subtract)
-    else: n = V("copy", [], T.tI[:], T.tgt[:])
-    if r > 0: x = V("ts", [sS], T.nI[:], T.S[:], T.en[:, r - 1:r], -1.0, A.add, A.add)
-    else: x = V("ts", [sS], T.nI[:], T.S[:], -1.0, None, A.add)
-    n = V("ts", [n], T.tJ[:], T.tI[:], 127, None, A.bitwise_and)
-    tb = V("ts", [n], T.tb[:], T.tJ[:], -1.0, -0.5, A.mult, A.add)
+    en = V("tt", [xs, cc], T.en[:], T.xs[:, 15:64:16], T.cc[:], A.add)
+    n0 = T.en[:, r - 1:r] if r > 0 else -1.0
+
+    x = V("scan", [en if r > 0 else sS], T.nI[:], T.l[:], T.zb[:, 0:256], n0, A.add, A.add)
+    n = V("ts", [], T.tI[:], T.tgt[:], n0, None, A.subtract)
     x = V("ts", [x], T.nA[:], T.nI[:], 24, None, A.bitwise_and)
+    n = V("ts", [n], T.tJ[:], T.tI[:], 127, None, A.bitwise_and)
     x = V("ts", [x], T.dm[:], T.nA[:], T.a8[:], None, A.is_equal)
+    tb = V("ts", [n], T.tb[:], T.tJ[:], -1.0, -0.5, A.mult, A.add)
     d = V("tt", [x, l], T.d[:, 32:288], T.dm[:], T.l[:], A.mult)
-    f = V("scan", [d], T.f[:], T.half[:], T.d[:], 0.0, A.mult, A.max)
-    b = V("tt", [], T.b[:], T.d[:, 0:288], T.d[:, 32:320], A.add)
-    x = V("tt", [b, f], T.tm[:], T.b[:], T.f[:, 17:305], A.max)
-    x = V("ts", [x], T.nd[:], T.tm[:], 0.25, None, A.is_ge)
-    tab = V("scan", [x], T.tab[:, 0:288], T.nd[:], T.zb[:, 0:288], 0.0, A.add, A.add)
     for k in range(2):
         al = S("sum", [sS, tb], T.junk[:, 288 * k:288 * k + 256], T.S[:], T.tb[:, k:k + 1], T.acl[:, k:k + 1])
-    NA = 6
+    f = V("scan", [d], T.f[:], T.half[:], T.d[:], 0.0, A.mult, A.max)
+    b = V("tt", [], T.b[:], T.d[:, 0:288], T.d[:, 32:320], A.add)
+    ci = V("ts", [al], T.cI[:], T.acl[:], -0.5, 128.0, A.mult, A.add)
+    x = V("tt", [b, f], T.tm[:], T.b[:], T.f[:, 17:305], A.max)
+    ji = V("ts", [ci], T.jI[:], T.cI[:], 15, None, A.bitwise_and)
+    x = V("ts", [x], T.nd[:], T.tm[:], 0.25, None, A.is_ge)
+    V("ts", [], T.l3[:], T.acl[:], -0.5, 143.0, A.mult, A.add)
+    tab = V("scan", [x], T.tab[:, 0:288], T.nd[:], T.zb[:, 0:288], 0.0, A.add, A.add)
+    junk = lambda k: T.junk[:, 288 * (k + 2):288 * (k + 3)]
     for k in range(NA):
-        ac = S("sum", [tab], T.junk[:, 288 * (k + 2):288 * (k + 3)], T.tab[:, 0:288], T.mbi[:, k:k + 1], T.acc[:, k:k + 1])
-    for k in range(NA, 9):
-        x = V("ts", [tab, kc], T.junk[:, 288 * (k + 2):288 * (k + 3)], T.tab[:, 0:288], T.mth[:, k:k + 1], None, A.is_le)
-    for k in range(NA, 9):
-        x = V("red", [x], T.cnt[:, k:k + 1], T.junk[:, 288 * (k + 2):288 * (k + 3)])
-    V("copy", [x], T.ofs[:, NA:9], T.cnt[:, NA:9])
-    x = V("ts", [ac], T.ofs[:, 0:NA], T.acc[:, 0:NA], -0.5, 144.0, A.mult, A.add)
-    for i, q in enumerate(others):
-        for k in range(4):
-            y = V("copy", [x], T["of%d" % i][32 * k:32 * k + 32, 0:9], T.ofs[32 * q:32 * q + 32, 0:9])
-        pq = V("copy", [y, hal, zc], U32(T["pkq%d" % i][:]), U32(T.winq[:]).indirect(T["of%d" % i][:, 0:9]))
-        ps = S("act", [y, hal, zc], T["pks%d" % i][:], T.wins[:].indirect(T["of%d" % i][:, 0:9]), F.Copy)
-        j = r if r < q else r - 1
-        rid, pid, _ = topo.addr(T.cores[q])
-        m = topo.mask(core, T.cores[q])
-        wait("p", [pq])
-        g.remote_dma(U8(T["lnq%d" % j][:]), U8(T["pkq%d" % i][:]), T.sem["cq%d" % j], T.sem.sent, pid, rid, m)
-        wait("p", [ps])
-        g.remote_dma(T["lns%d" % j][:], T["pks%d" % i][:], T.sem["cs%d" % j], T.sem.sent, pid, rid, m)
-        cnt["sent"] += 2 * ne
-
-    V("ts", [al], T.cI[:], T.acl[:], -0.5, 128.0, A.mult, A.add)
+        ac = S("sum", [tab], junk(k), T.tab[:, 0:288], T.mbi[:, k:k + 1], T.acc[:, k:k + 1])
+    V("ts", [ji], T.c3[:], T.jI[:], 0.0, 288.0, A.is_equal, A.mult)
+    V("ts", [], T.l4[:], T.acl[:], -0.5, 145.0, A.mult, A.add)
+    x = V("ts", [], T.c4[:], T.jI[:], 15.0, 288.0, A.is_equal, A.mult)
     V("ts", [], T.iof[:, 0:2], T.acl[:], -0.5, 144.0, A.mult, A.add)
     V("ts", [], T.iof[:, 2:4], T.acl[:], -0.5, 128.0, A.mult, A.add)
     V("ts", [], T.iof[:, 4:6], T.acl[:], -0.5, 160.0, A.mult, A.add)
-    V("ts", [], T.l3[:], T.acl[:], -0.5, 143.0, A.mult, A.add)
-    x = V("ts", [], T.l4[:], T.acl[:], -0.5, 145.0, A.mult, A.add)
-    x = V("ts", [x], T.jI[:], T.cI[:], 15, None, A.bitwise_and)
-    V("ts", [x], T.c3[:], T.jI[:], 0.0, 288.0, A.is_equal, A.mult)
-    x = V("ts", [], T.c4[:], T.jI[:], 15.0, 288.0, A.is_equal, A.mult)
     V("tt", [x], T.iof[:, 6:8], T.l3[:], T.c3[:], A.max)
     x = V("tt", [], T.iof[:, 8:10], T.l4[:], T.c4[:], A.max)
+    cm = [V("ts", [tab, kc], junk(k), T.tab[:, 0:288], T.mth[:, k:k + 1], None, A.is_le) for k in range(NA, 9)]
     io = V("copy", [x], T.io16[:], T.iof[:])
-    x = V("copy", [io, tab], T.g1[:], T.tab[:].indirect(T.io16[:]))
+    rd = lambda k: V("red", [cm[k - NA]], T.cnt[:, k:k + 1], junk(k))
+    for k in range(NA, 7): rd(k)
+    x = V("copy", [io], T.g1[:], T.tab[:].indirect(T.io16[:]))
+    rd(7)
     x = V("scan", [x], T.x1[:], T.ext[:], T.g1[:], 0.0, A.add, A.max)
+    y = rd(8)
     x = V("ts", [x], T.ix[:], T.x1[:, 15:160:16], T.corr[:], 0.0, A.subtract, A.max)
+    V("copy", [y], T.ofs[:, NA:9], T.cnt[:, NA:9])
     x = V("ts", [x], T.ixh[:], T.ix[:, 1:10:2], 256.0, None, A.mult)
+    y0 = V("ts", [ac], T.ofs[:, 0:NA], T.acc[:, 0:NA], -0.5, 144.0, A.mult, A.add)
     x = V("tt", [x], T.ixp[:], T.ix[:, 0:10:2], T.ixh[:], A.add)
-    x = V("copy", [x], T.idm[:, 0:5], T.ixp[:])
-    wait("p", [x])
-    to_all(T.idm[:, 0:5], [T.li[:, 5 * (r if r < q else r - 1):5 * (r if r < q else r - 1) + 5] for q in others], T.sem.idx)
-    for k in range(4):
-        y = V("copy", [io], T.ioo[32 * k:32 * k + 32, :], T.io16[32 * r:32 * r + 32, :])
-    pe = [V("copy", [y], U32(T.eq[:, 160 * r:160 * r + 160]), U32(T.winq[:]).indirect(T.ioo[:]))]
-    pf = [S("act", [y], T.es[:, 160 * r:160 * r + 160], T.wins[:].indirect(T.ioo[:]), F.Copy)]
-    for k in range(4):
-        x = V("ts", [en], T.gq[:, 8 * k:8 * k + 8], T.nP[:], T.en[:, k:k + 1], 640.0 if k == 3 else 160.0, A.is_ge, A.mult)
-    x = V("tt", [x], T.bq[:, 0:8], T.slot[:], T.gq[:, 0:8], A.add)
-    y = V("tt", [], T.bq[:, 8:16], T.gq[:, 8:16], T.gq[:, 16:24], A.add)
-    x = V("tt", [y], T.bq[:, 16:24], T.bq[:, 0:8], T.bq[:, 8:16], A.add)
-    x = V("tt", [x], T.bq[:, 24:32], T.bq[:, 16:24], T.gq[:, 24:32], A.max)
-    for k in range(5):
-        fo = V("ts", [x], T.fo[:, 8 * k:8 * k + 8], T.bq[:, 24:32], 32.0 * k, None, A.add)
-    for k in range(3):
-        e = min(1280, 512 * k + 512)
-        qw = V("quant", [ldw[k]], T.wq[:, 512 * k:e], T.ws[:, 512 * k:e], T.wt[:, 2048 * k:4 * e])
+    tk, pls = {}, []
 
+    def own(k): tk["own"] = V("copy", [io], T.ioo[32 * k:32 * k + 32, :], T.io16[32 * r:32 * r + 32, :])
+
+    def gq(k): tk["gq"] = V("ts", [en], T.gq[:, 8 * k:8 * k + 8], T.nP[:], T.en[:, k:k + 1], 640.0 if k == 3 else 160.0, A.is_gt, A.mult)
+    todo = [lambda: gq(0), lambda: gq(1), lambda: gq(2), lambda: gq(3), lambda: own(0), lambda: own(1), lambda: own(2), lambda: own(3)]
+
+    def fill(n):
+        for f in todo[:n]: f()
+        del todo[:n]
+    for dq in range(1, N):
+        q = (r + dq) % N
+        i, j = at(q, r), at(r, q)
+        for k in range(4):
+            y = V("copy", [y0], T["of%d" % i][32 * k:32 * k + 32, 0:9], T.ofs[32 * q:32 * q + 32, 0:9])
+            if dq == 1 and k == 0: x = V("copy", [x], T.idm[:, 0:5], T.ixp[:])
+        if dq == 1:
+            wait("p", [x])
+            send([(others, eng[q], T.sem.idx, T.idm[:, 0:5], [T.li[:, 5 * at(r, p):5 * at(r, p) + 5] for p in others])])
+        fill(2)
+        off = T["of%d" % i][:, 0:9]
+        pq = V("copy", [y, hal, zc], U32(T["pkq%d" % i][:]), U32(T.winq[:]).indirect(off))
+        ps = S("act", [y, hal, zc], T["pks%d" % i][:], T.wins[:].indirect(off), F.Copy)
+        pls.append(([q], eng[q][4 * dq - 4:4 * dq], T.sem["cs%d" % j], T["pks%d" % i][:], [T["lns%d" % j][:]]))
+        if dq == N - 1:
+            wait("p", [ps])
+            send(pls)
+        wait("p", [pq])
+        send([([q], eng[q], T.sem["cq%d" % j], U8(T["pkq%d" % i][:]), [U8(T["lnq%d" % j][:])])])
+    fill(8)
+    x = V("tt", [tk["gq"]], T.bq[:, 0:8], T.slot[:], T.gq[:, 0:8], A.add)
+    y = V("tt", [], T.bq[:, 8:16], T.gq[:, 8:16], T.gq[:, 16:24], A.add)
+    pe = [V("copy", [tk["own"]], U32(T.eq[:, 160 * r:160 * r + 160]), U32(T.winq[:]).indirect(T.ioo[:]))]
+    pf = [S("act", [tk["own"]], T.es[:, 160 * r:160 * r + 160], T.wins[:].indirect(T.ioo[:]), F.Copy)]
+    x = V("tt", [y], T.bq[:, 16:24], T.bq[:, 0:8], T.bq[:, 8:16], A.add)
+    V("quant", [ldw[1]], T.wq[:, W(1)], T.ws[:, W(1)], T.wt[:, W4(1)])
+    x = V("tt", [x], T.bq[:, 24:32], T.bq[:, 16:24], T.gq[:, 24:32], A.max)
     ix = ("idx", 3 * ne)
+    fo = lambda k: V("ts", [x], T.fo[:, 8 * k:8 * k + 8], T.bq[:, 24:32], 32.0 * k, None, A.add)
     for k in range(4):
-        x = V("copy", [ix], T.lb[32 * k:32 * k + 32, 0:15], T.li[32 * r:32 * r + 32, 0:15])
-    x = V("copy", [x], T.lbi[:, 0:15], T.lb[:, 0:15])
-    V("ts", [x], T.llo[:, 0:15], T.lbi[:, 0:15], 255, None, A.bitwise_and)
-    x = V("ts", [], T.lhi[:, 0:15], T.lbi[:, 0:15], 8, None, A.logical_shift_right)
-    V("copy", [x], T.lo[:, 0:30:2], T.llo[:, 0:15])
-    x = V("copy", [], T.lo[:, 1:30:2], T.lhi[:, 0:15])
-    for i, q in enumerate(others):
-        pe.append(V("copy", [x, ("cq%d" % i, ne)], U32(T.eq[:, 160 * q:160 * q + 160]), U32(T["lnq%d" % i][:]).indirect(T.lo[:, 10 * i:10 * i + 10])))
-        pf.append(S("act", [x, ("cs%d" % i, ne)], T.es[:, 160 * q:160 * q + 160], T["lns%d" % i][:].indirect(T.lo[:, 10 * i:10 * i + 10]), F.Copy))
+        z = V("copy", [ix], T.lb[32 * k:32 * k + 32, 0:15], T.li[32 * r:32 * r + 32, 0:15])
+    fo(0)
+    fo(1)
+    z = V("copy", [z], T.lbi[:, 0:15], T.lb[:, 0:15])
+    fo(2)
+    fo(3)
+    V("ts", [z], T.llo[:, 0:15], T.lbi[:, 0:15], 255, None, A.bitwise_and)
+    z = V("ts", [], T.lhi[:, 0:15], T.lbi[:, 0:15], 8, None, A.logical_shift_right)
+    fd = fo(4)
+    V("copy", [z], T.lo[:, 0:30:2], T.llo[:, 0:15])
+    z = V("copy", [], T.lo[:, 1:30:2], T.lhi[:, 0:15])
+    qw = V("quant", [ldw[2]], T.wq[:, W(2)], T.ws[:, W(2)], T.wt[:, W4(2)])
+    for dq in range(1, N):
+        q = (r - dq) % N
+        i = at(q, r)
+        off = T.lo[:, 10 * i:10 * i + 10]
+        pe.append(V("copy", [z, ("cq%d" % i, ne)], U32(T.eq[:, 160 * q:160 * q + 160]), U32(T["lnq%d" % i][:]).indirect(off)))
+        pf.append(S("act", [z, ("cs%d" % i, 4)], T.es[:, 160 * q:160 * q + 160], T["lns%d" % i][:].indirect(off), F.Copy))
+
     for k in range(5):
         lo, hi = 128 * k, 128 * k + 128
-        a = V("copy", [pe[-1], fo], U32(T.xfq[:, lo:hi]), U32(T.eq[:]).indirect(T.fo[:, 8 * k:8 * k + 8]))
-        b = S("act", [pf[-1], fo], T.xfs[:, lo:hi], T.es[:].indirect(T.fo[:, 8 * k:8 * k + 8]), F.Copy)
+        a = V("copy", [pe[-1], fd], U32(T.xfq[:, lo:hi]), U32(T.eq[:]).indirect(T.fo[:, 8 * k:8 * k + 8]))
+        b = S("act", [pf[-1], fd], T.xfs[:, lo:hi], T.es[:].indirect(T.fo[:, 8 * k:8 * k + 8]), F.Copy)
         ms = []
         for o in range(2):
             w = 128 * (2 * k + o)
             ms.append(op("t", "mm", [a, b, qw], T.yp[:, 512 * o:512 * o + 128], T.wq[:, w:w + 128], T.ws[:, w:w + 128],
                          T.xfq[:, lo:hi], T.xfs[:, lo:hi], k == 0, k == 4))
     x = V("copy", [ms[0]], T.ys[:, 0:128], T.yp[:, 0:128])
-    s0 = dma("s", "st0", [x], T.y[:, 0:128], T.ys[:, 0:128])
+    dma("s", "st0", [x], T.y[:, 0:128], T.ys[:, 0:128])
     x = S("act", [ms[1]], T.ys[:, 128:256], T.yp[:, 512:640], F.Copy)
-    s1 = dma("a", "st1", [x], T.y[:, 128:256], T.ys[:, 128:256])
+    dma("a", "st1", [x], T.y[:, 128:256], T.ys[:, 128:256])
     wait("p", [(k, n) for k, n in cnt.items()])
     wait("p", [hal, inf, ix])

@@ -3,9 +3,11 @@ from concourse.mybir import dt, AluOpType, ActivationFunctionType, AxisListType
 
 A = AluOpType
 F = ActivationFunctionType
-CAP = 144
-NA = 7
 CODE = "float8_e4m3fn_x4"
+X0 = 128
+ZC = 448
+RG = 176
+KPOS = [3, 0, 4, 1, 2]
 
 
 def sb(n, d="float32"): return ("sbuf", [128, n], d)
@@ -13,34 +15,32 @@ def sb(n, d="float32"): return ("sbuf", [128, n], d)
 
 BF, I32, U16 = "bfloat16", "int32", "uint16"
 SCRATCH = {
-    "ut": sb(512, BF), "xt": sb(1024, BF), "wt": sb(5120, BF), "zt": sb(640, BF), "zb": sb(320, BF),
+    "ut": sb(512, BF), "xt": sb(1024, BF), "wt": sb(5120, BF), "zt": sb(640, BF),
     "uq": sb(128, CODE), "us": sb(128, "uint8"), "urq": sb(128, CODE), "urs": sb(128, "uint8"),
-    "winq": sb(416, CODE), "wins": sb(416, "uint8"),
+    "winq": sb(544, CODE), "wins": sb(544, "uint8"),
     "wq": sb(1280, CODE), "ws": sb(1280, "uint8"),
-    "eq": sb(800, CODE), "es": sb(800, "uint8"),
+    "eq": sb(4 * RG + 160, CODE), "es": sb(4 * RG + 160, "uint8"),
     "xfq": sb(640, CODE), "xfs": sb(640, "uint8"),
     "off0": sb(8, U16), "ys": sb(256),
     "sc": ("psum", [128, 512], "float32"), "yp": ("psum", [128, 1024], "float32"),
-    "pI": sb(1, I32), "pm": sb(4, I32), "p16": sb(1), "a8": sb(1), "bc": sb(4), "corr": sb(1),
-    "i64": sb(8), "i16": sb(8), "y16": sb(10), "tgt": sb(2), "nP": sb(8), "slot": sb(8), "mth": sb(10), "mbi": sb(10),
-    "tt16": sb(160), "ext1": sb(160), "ext": sb(160), "half": sb(320, BF),
-    "s": sb(256, BF), "hp": sb(288, BF), "vp": sb(288, BF), "m1": sb(256, BF), "m2": sb(256, BF), "m3": sb(256, BF), "gh": sb(256, BF),
-    "l": sb(256, BF), "pl": sb(256, BF), "q0": sb(16, BF), "q15": sb(16, BF), "inf": sb(160, BF),
-    "dd": sb(48), "dq": sb(48), "e9": sb(48), "e11": sb(48), "eb": sb(64), "et": sb(64), "xs": sb(64), "cc": sb(4), "en": sb(4),
-    "S": sb(256, BF), "tI": sb(2, I32), "tJ": sb(2, I32), "tb": sb(2), "nI": sb(256, I32), "nA": sb(256, I32), "dm": sb(256, BF),
-    "d": sb(320, BF), "f": sb(320, BF), "b": sb(288, BF), "tm": sb(288, BF), "nd": sb(288, BF), "tab": sb(320, BF),
-    "junk": sb(3200, BF), "acl": sb(2), "acc": sb(10), "cnt": sb(10), "ofs": sb(10, U16),
-    "cI": sb(2, I32), "jI": sb(2, I32), "l3": sb(2), "l4": sb(2), "c3": sb(2), "c4": sb(2),
-    "iof": sb(10), "io16": sb(10, U16), "ioo": sb(10, U16), "g1": sb(160), "x1": sb(160), "ix": sb(10), "ixh": sb(5), "ixp": sb(5),
-    "idm": sb(8, U16), "li": sb(16, U16), "lb": sb(16, U16), "lbi": sb(16, I32), "llo": sb(16, I32), "lhi": sb(16, I32), "lo": sb(32, U16),
-    "gq": sb(32), "bq": sb(32), "fo": sb(40, U16),
+    "pI": sb(1, I32), "pm": sb(4, I32), "p16": sb(1), "a8": sb(1), "bc": sb(4), "bE": sb(1), "x8": sb(1),
+    "i64": sb(8), "i16": sb(8), "tgt": sb(2), "nP": sb(8), "slot": sb(8), "cE": sb(8), "kk": sb(8),
+    "half": sb(256, BF), "zb": sb(256, BF), "two": sb(16, BF), "ip": sb(16),
+    "P": sb(256, BF), "n2": sb(256, BF), "hp": sb(288, BF), "vp": sb(256, BF), "vn": sb(272, BF), "m1": sb(256, BF), "gh": sb(256, BF),
+    "v2": sb(256, BF), "o2": sb(256, BF), "l": sb(272, BF), "S": sb(272, BF), "ob": sb(32, BF), "e": sb(32, BF),
+    "pk": sb(48), "bd": sb(16), "ub": sb(32, I32), "u2": sb(32, I32), "fb": sb(16, I32), "f2": sb(16, I32),
+    "inf": sb(32, BF), "en": sb(6), "nen": sb(6), "tI": sb(2, I32), "tJ": sb(2, I32), "tb": sb(2),
+    "junk": sb(544, BF), "acl": sb(2), "cI": sb(2, I32), "jI": sb(2, I32), "cf": sb(6), "iof": sb(12),
+    "eI": sb(1, I32), "eJ": sb(1, I32), "eT": sb(1), "eB": sb(16), "eR": sb(1),
+    "g": sb(48), "ga": sb(8), "gb": sb(8), "gc1": sb(8), "gs": sb(8), "b0": sb(8), "b1": sb(8), "bb": sb(8), "uu": sb(8), "b2": sb(8),
+    "fo": sb(8, U16), "fu": sb(8, U16), "ioo": sb(12, U16), "spo": sb(12),
 }
 for _i in range(3):
-    SCRATCH["of%d" % _i] = sb(10, U16)
-    for _n in ("pk", "ln"):
-        SCRATCH["%sq%d" % (_n, _i)] = sb(CAP, CODE)
-        SCRATCH["%ss%d" % (_n, _i)] = sb(CAP, "uint8")
-SEMAPHORES = ["vc", "ac", "tc", "pc", "ldu", "ldx", "ldw0", "ldw1", "ldw2", "zc", "halo", "info", "idx",
+    SCRATCH["of%d" % _i] = sb(12, U16)
+    SCRATCH["sp%d" % _i] = sb(12)
+    SCRATCH["pkq%d" % _i] = sb(RG, CODE)
+    SCRATCH["pks%d" % _i] = sb(RG, "uint8")
+SEMAPHORES = ["vc", "ac", "tc", "pc", "ldu", "ldx", "ldw0", "ldw1", "ldw2", "halo", "bdr", "info", "flg",
               "cq0", "cq1", "cq2", "cs0", "cs1", "cs2", "sent", "st0", "st1"]
 
 
@@ -75,6 +75,7 @@ def rank_program(g, core, T, topo):
         elif name == "scan": i = q.tensor_tensor_scan(*args)
         elif name == "quant": i = q.quantize_mx(*args)
         elif name == "act": i = q.activation(*args)
+        elif name == "sign": i = q.activation(args[0], args[1], F.Sign, bias=args[2], scale=1.0)
         elif name == "sum": i = q.activation(args[0], args[1], F.Sign, bias=args[2], scale=1.0, accum_out=args[3])
         elif name == "mm": i = q.matmul_mx(*args)
         elif name == "iota": i = q.iota(*args)
@@ -107,220 +108,218 @@ def rank_program(g, core, T, topo):
     W = lambda k: slice(512 * k, min(1280, 512 * k + 512))
     W4 = lambda k: slice(2048 * k, min(5120, 2048 * k + 2048))
 
+    up, dn = r > 0, r < N - 1
+    ex_out = r in (0, 1)
+    L = 272 if r == 0 else 256
     ldu = dma("a", "ldu", [], T.ut[:, 0:8], T.u[:, 0:8])
     ldx = dma("s", "ldx", [], T.xt[:], T.x[:])
     mu = V("memset", [], T.ut[:, 8:512], 0.0)
     mo = V("memset", [], T.off0[:], 0)
-    V("memset", [], T.hp[:, 0:16], 1.0)
-    V("memset", [], T.vp[:, 0:16], 1.0)
-    cv = V("memset", [], T.vp[:, 256:272], 1.0)
-    V("memset", [], T.zb[:], 0.0)
-    mz = V("memset", [], T.zt[:], 0.0)
-    ch = V("memset", [], T.half[:], 0.5)
-    qz = V("quant", [mz], T.winq[:, 288:416], T.wins[:, 288:416], T.zt[:, 0:512])
-    k0 = op("p", "iota", [], T.pI[:], [[0, 1]], 0, 1)
+    kp = op("p", "iota", [], T.pI[:], [[0, 1]], 0, 1)
     op("p", "iotaf", [], T.i64[:], [[64, 8]], 0, 0)
     op("p", "iotaf", [], T.i16[:], [[0, 4], [16, 2]], 0, 0)
-    op("p", "iotaf", [], T.y16[:], [[16, 10]], 0, 0)
-    k4 = op("p", "iotaf", [], T.tt16[:], [[0, 10], [1, 16]], 0, 0)
-    ldw = [dma("s", "ldw0", [ldx], T.wt[:, W4(0)], T.w[:, W4(0)])]
+    op("p", "iotaf", [], T.kk[:, 0:3], [[-2, 3]], -2 * (X0 - 1) - L, 0)
+    kg = op("p", "iotaf", [], T.kk[:, 3:5], [[-64, 2]], -2 * (X0 - 16) - L, 0)
+    V("memset", [], T.zb[:], 0.0)
+    V("memset", [], T.vn[:, 0:16], -3.0)
+    V("memset", [], T.vn[:, 256:272], -3.0)
+    V("memset", [], T.half[:], 0.5)
+    V("memset", [], T.cf[:, 2:4], 0.0)
+    k2 = V("memset", [], T.two[:], 2.0)
+    mz = V("memset", [], T.zt[:], 0.0)
+    V("ts", [kp], T.pm[:, 3:4], T.pI[:], 5, None, A.logical_shift_right)
+    V("ts", [], T.pm[:, 0:1], T.pI[:], 15, None, A.bitwise_and)
+    V("ts", [], T.pm[:, 1:2], T.pI[:], 7, None, A.bitwise_and)
+    kc = V("ts", [], T.pm[:, 2:3], T.pI[:], 3, 1, A.logical_shift_right, A.bitwise_and)
 
     qu = V("quant", [ldu, mu], T.uq[:], T.us[:], T.ut[:])
     pu = V("copy", [qu, mo], U32(T.urq[:]), U32(T.uq[:]).indirect(T.off0[:]))
     pv = S("act", [qu, mo], T.urs[:], T.us[:].indirect(T.off0[:]), F.Copy)
-    qx = V("quant", [ldx], T.winq[:, 16:272], T.wins[:, 16:272], T.xt[:])
-    mm = op("t", "mm", [pu, pv, qx], T.sc[:, 0:256], T.urq[:], T.urs[:], T.winq[:, 16:272], T.wins[:, 16:272], True, True)
+    qx = V("quant", [ldx], T.winq[:, X0:X0 + 256], T.wins[:, X0:X0 + 256], T.xt[:])
+    mm = op("t", "mm", [pu, pv, qx], T.sc[:, 0:256], T.urq[:], T.urs[:], T.winq[:, X0:X0 + 256], T.wins[:, X0:X0 + 256], True, True)
+    ldw = [dma("s", "ldw0", [ldx], T.wt[:, W4(0)], T.w[:, W4(0)])]
 
-    nb = ([(r - 1, 16, 272)] if r > 0 else []) + ([(r + 1, 256, 0)] if r < N - 1 else [])
+    nb = ([(r - 1, X0, X0 + 256)] if up else []) + ([(r + 1, X0 + 240, X0 - 16)] if r == N - 2 else [])
 
     def strips(view):
-        send([([q], eng[q][k * (ne // 2):(k + 1) * (ne // 2)], T.sem.halo, view(src, src + 16), [view(dst, dst + 16)])
-              for k, (q, src, dst) in enumerate(nb)])
+        if nb:
+            send([([q], eng[q][k * (ne // 2):(k + 1) * (ne // 2)], T.sem.halo, view(src, src + 16), [view(dst, dst + 16)])
+                  for k, (q, src, dst) in enumerate(nb)])
     wait("p", [qx])
     strips(lambda a, b: U8(T.winq[:, a:b]))
-    hal, zc = ("halo", 2 * len(nb) * (ne // 2)), None
-    if len(nb) == 1:
-        to = 0 if r == 0 else 272
-        dma("s", "zc", [qz], U8(T.winq[:, to:to + 16]), U8(T.winq[:, 288:304]))
-        zc = dma("s", "zc", [], T.wins[:, to:to + 16], T.wins[:, 288:304])
+    hal = ("halo", 2 * (ne // 2))
 
-    s = S("act", [mm], T.s[:], T.sc[:, 0:256], F.Sign)
-    h = V("tt", [s, mm], T.hp[:, 16:271], T.s[:, 0:255], T.sc[:, 1:256], A.mult)
-    v = V("tt", [], T.vp[:, 16:256], T.s[:, 0:240], T.sc[:, 16:256], A.mult)
-    h = V("memset", [h], T.hp[:, 31:272:16], 1.0)
-    v = V("tt", [v, cv], T.m2[:], T.vp[:, 16:272], T.vp[:, 0:256], A.min)
-    h = V("ts", [h], T.m1[:], T.hp[:, 16:272], 0.0, -1.0, A.is_lt, A.mult)
-    h = V("scan", [h, ch], T.gh[:], T.half[:, 0:256], T.m1[:], 0.0, A.mult, A.min)
-    h = V("tt", [h, v], T.m3[:], T.gh[:], T.m2[:], A.min)
-    l = V("ts", [h], T.l[:], T.m3[:], -0.375, None, A.is_le)
-    pl = V("scan", [l], T.pl[:], T.l[:], T.zb[:, 0:256], 0.0, A.add, A.add)
-    o = 40 * r
-    V("ts", [], T.q15[:], T.l[:, 240:256], -2.0, 6.0, A.mult, A.add)
-    t = V("ts", [], T.q0[:], T.l[:, 0:16], -1.0, 5.0, A.mult, A.add)
-    V("copy", [pl], T.inf[:, o + 16:o + 18], T.pl[:, 254:256])
-    V("tt", [t], T.inf[:, o + 18:o + 34], T.q15[:], T.s[:, 240:256], A.mult)
-    t = V("tt", [], T.inf[:, o:o + 16], T.q0[:], T.s[:, 0:16], A.mult)
-    a, b = o + (16 if r == 0 else 0), o + (18 if r == N - 1 else 34)
-    wait("p", [t])
-    send([(others, eng[others[0]], T.sem.info, T.inf[:, a:b], [T.inf[:, a:b]] * 3)])
-    inf = ("info", 3 * ne)
+    kip = V("scan", [k2], T.ip[:], T.two[:], T.zb[:, 0:16], 2.0 ** -16, A.mult, A.add)
+    V("ts", [kc], T.bc[:, 0:1], T.pm[:, 2:3], 32.0, None, A.mult)
+    k = V("copy", [kc], T.bc[:, 1:2], T.pm[:, 1:2])
+    V("ts", [kc], T.p16[:], T.pm[:, 0:1], 2.0 / RG, 4 + 0.5 / RG, A.mult, A.add)
+    V("ts", [kc], T.a8[:], T.pm[:, 3:4], 8.0, None, A.mult)
+    V("ts", [kc], T.x8[:], T.pm[:, 2:3], -8.0 / RG, 64.0 / RG, A.mult, A.add)
+
+    if up: V("ts", [mm], T.P[:, 0:16], T.sc[:, 0:16], 0.0, None, A.is_gt)
+    if dn: V("ts", [mm], T.P[:, 240:256], T.sc[:, 240:256], 0.0, None, A.is_gt)
+    a, b = (16 if up else 0), (240 if dn else 256)
+    kr = ("vc", cnt["vc"])
+    p = V("ts", [mm], T.P[:, a:b], T.sc[:, a:b], 0.0, None, A.is_gt)
+    if up: ka = V("scan", [kr], T.pk[:, 0:16], T.two[:], T.P[:, 0:16], 2.0 ** -17, A.mult, A.add)
+    if dn: ka = V("scan", [kr], T.pk[:, 16:32], T.two[:], T.P[:, 240:256], 2.0 ** -17, A.mult, A.add)
+    n2 = V("ts", [p], T.n2[:], T.P[:], -2.0, None, A.add)
+    wait("p", [ka])
+    send(([([r - 1], eng[r - 1][:ne // 2], T.sem.bdr, T.pk[:, 15:16], [T.bd[:, 4:5]])] if up else [])
+         + ([([r + 1], eng[r + 1][ne // 2:], T.sem.bdr, T.pk[:, 31:32], [T.bd[:, 0:1]])] if dn else []))
     strips(lambda a, b: T.wins[:, a:b])
-    ldw += [dma("s", "ldw%d" % k, [t], T.wt[:, W4(k)], T.w[:, W4(k)]) for k in (1, 2)]
+    h = V("scan", [n2], T.hp[:, 16:271], T.P[:, 0:255], T.n2[:, 1:256], -100.0, A.max, A.add)
+    v = V("scan", [], T.vp[:, 0:240], T.P[:, 0:240], T.n2[:, 16:256], -100.0, A.max, A.add)
+    h = V("memset", [h], T.hp[:, 31:272:16], 0.0)
+    v = V("ts", [v], T.vn[:, 16:256], T.vp[:, 0:240], -1.0, -3.0, A.is_equal, A.add)
+    h = V("ts", [h], T.m1[:], T.hp[:, 16:272], -1.0, None, A.is_equal)
+    v = V("scan", [v], T.v2[:], T.vn[:, 16:272], T.vn[:, 0:256], -100.0, A.max, A.add)
+    h = V("scan", [h], T.gh[:], T.half[:], T.m1[:], 0.0, A.mult, A.max)
+    if up: V("copy", [], T.ob[:, 0:16], T.P[:, 0:16])
+    h = V("scan", [h, v], T.o2[:], T.gh[:], T.v2[:], -100.0, A.max, A.add)
+    if dn: V("copy", [], T.ob[:, 16:32], T.P[:, 240:256])
+    l = V("ts", [h], T.l[:, 0:256], T.o2[:], -5.6, None, A.is_gt)
+    ldw.append(dma("s", "ldw1", [h], T.wt[:, W4(1)], T.w[:, W4(1)]))
 
-    V("ts", [k0], T.pm[:, 0:1], T.pI[:], 15, None, A.bitwise_and)
-    V("ts", [], T.pm[:, 1:2], T.pI[:], 7, None, A.bitwise_and)
-    V("ts", [], T.pm[:, 2:3], T.pI[:], 3, 1, A.logical_shift_right, A.bitwise_and)
-    k = V("ts", [], T.pm[:, 3:4], T.pI[:], 5, None, A.logical_shift_right)
-    V("memset", [], T.d[:, 0:32], 0.0)
-    V("copy", [k], T.p16[:], T.pm[:, 0:1])
-    V("ts", [], T.a8[:], T.pm[:, 3:4], 8.0, None, A.mult)
-    V("ts", [], T.corr[:], T.pm[:, 0:1], -256.0, 256.0 * 15 + 1, A.mult, A.add)
-    V("ts", [], T.bc[:, 0:1], T.pm[:, 2:3], 32.0, None, A.mult)
-    k = V("copy", [], T.bc[:, 1:2], T.pm[:, 1:2])
-    V("memset", [], T.d[:, 288:320], 0.0)
-    k1 = V("ts", [k4, k], T.mth[:], T.y16[:], T.p16[:], None, A.add)
     k = V("tt", [k], T.bc[:, 2:3], T.bc[:, 0:1], T.bc[:, 1:2], A.add)
-    V("memset", [], T.tab[:, 288:320], float(CAP))
-    V("ts", [k1], T.mbi[:], T.mth[:], -1.0, -0.5, A.mult, A.add)
+    V("ts", [kg], T.slot[:], T.i16[:], 2.0 / RG, T.p16[:], A.mult, A.add)
+    V("ts", [], T.cE[:], T.i16[:], -1.0 / RG, T.x8[:], A.mult, A.add)
     k = V("tt", [k], T.bc[:, 3:4], T.bc[:, 2:3], T.a8[:], A.add)
-    k1 = V("ts", [], T.ext1[:], T.tt16[:], T.p16[:], 512.0, A.is_gt, A.mult)
-    V("memset", [], T.eb[:, 48:64], 0.0)
-    V("memset", [], T.et[:, 0:16], 0.0)
-    V("ts", [k], T.tgt[:], T.i64[:, 0:2], T.bc[:, 3:4], 1023.0, A.add, A.add)
-    k1 = V("ts", [k1], T.ext[:], T.ext1[:], -256.0, None, A.add)
     V("ts", [], T.nP[:], T.i64[:], T.bc[:, 2:3], 8.0 * r, A.add, A.add)
-    V("ts", [], T.slot[:], T.i16[:], T.p16[:], None, A.add)
-    kc = V("memset", [k1], T.ext[:, 0:160:16], -5120.0)
-    V("quant", [], T.eq[:, 640:800], T.es[:, 640:800], T.zt[:])
-    V("quant", [ldw[0]], T.wq[:, W(0)], T.ws[:, W(0)], T.wt[:, W4(0)])
+    kt = V("ts", [k], T.tgt[:], T.i64[:, 0:2], T.bc[:, 3:4], 1023.0, A.add, A.add)
+    if ex_out: V("ts", [], T.bE[:], T.a8[:], T.bc[:, 1:2], 1023.0, A.add, A.add)
+    for a in ([0, 400] if dn else [384]):
+        qz = V("quant", [mz], T.winq[:, a:a + 128], T.wins[:, a:a + 128], T.zt[:, 0:512])
 
-    for k in range(3):
-        x = V("tt", [inf, t, kc], T.dd[:, 16 * k:16 * k + 16], T.inf[:, 40 * k + 18:40 * k + 34], T.inf[:, 40 * k + 40:40 * k + 56], A.subtract)
-    cc = V("scan", [], T.cc[:], T.inf[:, 17:160:40], T.zb[:, 0:4], -1.0, A.add, A.add)
-    x = V("tt", [x], T.dq[:], T.dd[:], T.dd[:], A.mult)
-    V("ts", [x], T.e9[:], T.dq[:], 81.0, None, A.is_equal)
-    y = V("ts", [], T.e11[:], T.dq[:], 121.0, None, A.is_equal)
-    eb = V("ts", [], T.eb[:, 0:48], T.dq[:], 95.0, None, A.is_ge)
-    et = V("tt", [y], T.et[:, 16:64], T.e9[:], T.e11[:], A.add)
-    if r < N - 1: l = V("tt", [eb, t], T.l[:, 240:256], T.l[:, 240:256], T.eb[:, 16 * r:16 * r + 16], A.add)
-    if r > 0: l = V("tt", [et, t], T.l[:, 0:16], T.l[:, 0:16], T.et[:, 16 * r:16 * r + 16], A.add)
-    xs = V("scan", [et], T.xs[:], T.eb[:], T.et[:], 0.0, A.add, A.add)
-    sS = V("scan", [l], T.S[:], T.l[:], T.zb[:, 0:256], 0.0, A.add, A.add)
-    en = V("tt", [xs, cc], T.en[:], T.xs[:, 15:64:16], T.cc[:], A.add)
-    n0 = T.en[:, r - 1:r] if r > 0 else -1.0
+    n0 = T.en[:, r - 1:r] if up else -1.0
+    mine = [lambda d: V("ts", [d], T.tI[:], T.tgt[:], n0, None, A.subtract),
+            lambda d: V("ts", [d], T.tJ[:], T.tI[:], 127, None, A.bitwise_and),
+            lambda d: V("ts", [d], T.tb[:], T.tJ[:], -1.0, -0.5, A.mult, A.add)]
+    if r == 0:
+        m = kt
+        for f in mine: m = f(m)
 
-    x = V("scan", [en if r > 0 else sS], T.nI[:], T.l[:], T.zb[:, 0:256], n0, A.add, A.add)
-    n = V("ts", [], T.tI[:], T.tgt[:], n0, None, A.subtract)
-    x = V("ts", [x], T.nA[:], T.nI[:], 24, None, A.bitwise_and)
-    n = V("ts", [n], T.tJ[:], T.tI[:], 127, None, A.bitwise_and)
-    x = V("ts", [x], T.dm[:], T.nA[:], T.a8[:], None, A.is_equal)
-    tb = V("ts", [n], T.tb[:], T.tJ[:], -1.0, -0.5, A.mult, A.add)
-    d = V("tt", [x, l], T.d[:, 32:288], T.dm[:], T.l[:], A.mult)
-    for k in range(2):
-        al = S("sum", [sS, tb], T.junk[:, 288 * k:288 * k + 256], T.S[:], T.tb[:, k:k + 1], T.acl[:, k:k + 1])
-    f = V("scan", [d], T.f[:], T.half[:], T.d[:], 0.0, A.mult, A.max)
-    b = V("tt", [], T.b[:], T.d[:, 0:288], T.d[:, 32:320], A.add)
-    ci = V("ts", [al], T.cI[:], T.acl[:], -0.5, 128.0, A.mult, A.add)
-    x = V("tt", [b, f], T.tm[:], T.b[:], T.f[:, 17:305], A.max)
-    ji = V("ts", [ci], T.jI[:], T.cI[:], 15, None, A.bitwise_and)
-    x = V("ts", [x], T.nd[:], T.tm[:], 0.25, None, A.is_ge)
-    V("ts", [], T.l3[:], T.acl[:], -0.5, 143.0, A.mult, A.add)
-    tab = V("scan", [x], T.tab[:, 0:288], T.nd[:], T.zb[:, 0:288], 0.0, A.add, A.add)
-    junk = lambda k: T.junk[:, 288 * (k + 2):288 * (k + 3)]
-    for k in range(NA):
-        ac = S("sum", [tab], junk(k), T.tab[:, 0:288], T.mbi[:, k:k + 1], T.acc[:, k:k + 1])
-    V("ts", [ji], T.c3[:], T.jI[:], 0.0, 288.0, A.is_equal, A.mult)
-    V("ts", [], T.l4[:], T.acl[:], -0.5, 145.0, A.mult, A.add)
-    x = V("ts", [], T.c4[:], T.jI[:], 15.0, 288.0, A.is_equal, A.mult)
-    V("ts", [], T.iof[:, 0:2], T.acl[:], -0.5, 144.0, A.mult, A.add)
-    V("ts", [], T.iof[:, 2:4], T.acl[:], -0.5, 128.0, A.mult, A.add)
-    V("ts", [], T.iof[:, 4:6], T.acl[:], -0.5, 160.0, A.mult, A.add)
-    V("tt", [x], T.iof[:, 6:8], T.l3[:], T.c3[:], A.max)
-    x = V("tt", [], T.iof[:, 8:10], T.l4[:], T.c4[:], A.max)
-    cm = [V("ts", [tab, kc], junk(k), T.tab[:, 0:288], T.mth[:, k:k + 1], None, A.is_le) for k in range(NA, 9)]
-    io = V("copy", [x], T.io16[:], T.iof[:])
-    rd = lambda k: V("red", [cm[k - NA]], T.cnt[:, k:k + 1], junk(k))
-    for k in range(NA, 7): rd(k)
-    x = V("copy", [io], T.g1[:], T.tab[:].indirect(T.io16[:]))
-    rd(7)
-    x = V("scan", [x], T.x1[:], T.ext[:], T.g1[:], 0.0, A.add, A.max)
-    y = rd(8)
-    x = V("ts", [x], T.ix[:], T.x1[:, 15:160:16], T.corr[:], 0.0, A.subtract, A.max)
-    V("copy", [y], T.ofs[:, NA:9], T.cnt[:, NA:9])
-    x = V("ts", [x], T.ixh[:], T.ix[:, 1:10:2], 256.0, None, A.mult)
-    y0 = V("ts", [ac], T.ofs[:, 0:NA], T.acc[:, 0:NA], -0.5, 144.0, A.mult, A.add)
-    x = V("tt", [x], T.ixp[:], T.ix[:, 0:10:2], T.ixh[:], A.add)
-    tk, pls = {}, []
+    bdr = ("bdr", (ne // 2) * len([q for q in (r - 1, r + 1) if 0 <= q < N]))
+    a, b = (0 if up else 16), (32 if dn else 16)
+    if up: x = V("ts", [bdr, kip], T.ub[:, 0:16], T.ip[:], T.bd[:, 0:1], -0.5, A.mult, A.add)
+    if dn: x = V("ts", [bdr, kip], T.ub[:, 16:32], T.ip[:], T.bd[:, 4:5], -0.5, A.mult, A.add)
+    x = V("ts", [x], T.u2[:, a:b], T.ub[:, a:b], 1, None, A.bitwise_and)
+    x = V("tt", [x], T.e[:, a:b], T.u2[:, a:b], T.ob[:, a:b], A.not_equal)
+    if up: l = V("tt", [x], T.l[:, 0:16], T.l[:, 0:16], T.e[:, 0:16], A.max)
+    if dn: l = V("tt", [x], T.l[:, 240:256], T.l[:, 240:256], T.e[:, 16:32], A.max)
+    sS = V("scan", [l], T.S[:, 0:256], T.l[:, 0:256], T.zb[:], 0.0, A.add, A.add)
+    if r in (1, 2): V("scan", [], T.pk[:, 32:48], T.two[:], T.l[:, 0:16], 2.0 ** -17, A.mult, A.add)
+    t = V("copy", [sS], T.inf[:, 8 * r:8 * r + 2], T.S[:, 15:256:240])
+    wait("p", [t])
+    e0 = eng[others[0]]
+    nB = lambda q: ne // 2 if q in (1, 2) else ne
+    send([(others, e0[:nB(r)], T.sem.info, T.inf[:, 8 * r:8 * r + 2], [T.inf[:, 8 * r:8 * r + 2]] * 3)]
+         + ([([r - 1], e0[ne // 2:], T.sem.flg, T.pk[:, 47:48], [T.bd[:, 8:9]])] if r in (1, 2) else []))
+    inf = ("info", sum(nB(q) for q in others))
+    flg = ("flg", ne // 2) if ex_out else None
+    ldw.append(dma("s", "ldw2", [t], T.wt[:, W4(2)], T.w[:, W4(2)]))
+    ze = V("quant", [], T.eq[:, 4 * RG:4 * RG + 160], T.es[:, 4 * RG:4 * RG + 160], T.zt[:])
+    for c in (0, 1): V("quant", [ldw[c]], T.wq[:, W(c)], T.ws[:, W(c)], T.wt[:, W4(c)])
 
-    def own(k): tk["own"] = V("copy", [io], T.ioo[32 * k:32 * k + 32, :], T.io16[32 * r:32 * r + 32, :])
+    def ends(d): return V("scan", [inf, t], T.en[:, 0:4], T.inf[:, 1:32:8], T.zb[:, 0:4], -1.0, A.add, A.add)
 
-    def gq(k): tk["gq"] = V("ts", [en], T.gq[:, 8 * k:8 * k + 8], T.nP[:], T.en[:, k:k + 1], 640.0 if k == 3 else 160.0, A.is_gt, A.mult)
-    todo = [lambda: gq(0), lambda: gq(1), lambda: gq(2), lambda: gq(3), lambda: own(0), lambda: own(1), lambda: own(2), lambda: own(3)]
+    row16 = [lambda d: V("ts", [flg], T.fb[:], T.ip[:], T.bd[:, 8:9], -0.5, A.mult, A.add),
+             lambda d: V("ts", [d], T.f2[:], T.fb[:], 1, None, A.bitwise_and),
+             lambda d: V("copy", [d], T.l[:, 256:272], T.f2[:]),
+             lambda d: V("scan", [d], T.S[:, 256:272], T.l[:, 256:272], T.zb[:, 0:16], T.S[:, 255:256], A.add, A.add)]
+    if r == 0:
+        x = None
+        for f in row16: x = f(x)
+        sS = x
+    else:
+        x = m = None
+        for i, f in enumerate([ends] + mine):
+            if r == 1 and i: x = row16[i - 1](x)
+            m = f(m)
+            if i == 0: en = m
+    for c in range(2):
+        al = S("sum", [sS, m], T.junk[:, 272 * c:272 * c + L], T.S[:, 0:L], T.tb[:, c:c + 1], T.acl[:, c:c + 1])
+    if r == 0: en = ends(None)
+    if r == 1: x = row16[3](x)
+    if ex_out:
+        x = V("ts", [en, x], T.eI[:], T.bE[:], T.en[:, r:r + 1], None, A.subtract)
+        x = V("ts", [x], T.eJ[:], T.eI[:], 31, None, A.bitwise_and)
+        x = V("ts", [x], T.eT[:], T.eJ[:], T.S[:, 255:256], None, A.add)
+        x = V("ts", [x], T.eB[:], T.S[:, 256:272], T.eT[:], None, A.is_le)
+        x = V("red", [x], T.eR[:], T.eB[:])
+        V("ts", [x], T.iof[:, 10:11], T.eR[:], X0 + 240.0, None, A.add)
+    else: V("tt", [en], T.en[:, 4:6], T.en[:, 0:2], T.inf[:, 8:17:8], A.add)
+    x = V("ts", [al], T.cI[:], T.acl[:], -0.5, L / 2.0, A.mult, A.add)
+    V("ts", [], T.iof[:, 0:10:2], T.kk[:, 0:5], T.acl[:, 0:1], -0.5, A.add, A.mult)
+    x = V("ts", [x], T.jI[:], T.cI[:], 15, None, A.bitwise_and)
+    V("ts", [], T.iof[:, 1:10:2], T.kk[:, 0:5], T.acl[:, 1:2], -0.5, A.add, A.mult)
+    V("ts", [x], T.cf[:, 0:2], T.jI[:], 0.0, float(ZC), A.is_equal, A.mult)
+    x = V("ts", [], T.cf[:, 4:6], T.jI[:], 15.0, float(ZC), A.is_equal, A.mult)
+    io = V("tt", [x], T.iof[:, 0:6], T.iof[:, 0:6], T.cf[:], A.max)
 
-    def fill(n):
-        for f in todo[:n]: f()
-        del todo[:n]
-    for dq in range(1, N):
-        q = (r + dq) % N
+    def nio(q): return 11 if r == 1 or (r == 0 and q < 2) else 10
+    def block(t, k, q): return t[32 * k:32 * k + 32, 0:nio(q)]
+    def spread(q, out): return [S("act", [io], block(out, k, q), block(T.iof, q, q), F.Copy) for k in range(4)][-1]
+    pls, pss = [], []
+    to = [(r + dq) % N for dq in range(1, N)]
+    for n, q in enumerate(to):
         i, j = at(q, r), at(r, q)
-        for k in range(4):
-            y = V("copy", [y0], T["of%d" % i][32 * k:32 * k + 32, 0:9], T.ofs[32 * q:32 * q + 32, 0:9])
-            if dq == 1 and k == 0: x = V("copy", [x], T.idm[:, 0:5], T.ixp[:])
-        if dq == 1:
-            wait("p", [x])
-            send([(others, eng[q], T.sem.idx, T.idm[:, 0:5], [T.li[:, 5 * at(r, p):5 * at(r, p) + 5] for p in others])])
-        fill(2)
-        off = T["of%d" % i][:, 0:9]
-        pq = V("copy", [y, hal, zc], U32(T["pkq%d" % i][:]), U32(T.winq[:]).indirect(off))
-        ps = S("act", [y, hal, zc], T["pks%d" % i][:], T.wins[:].indirect(off), F.Copy)
-        pls.append(([q], eng[q][4 * dq - 4:4 * dq], T.sem["cs%d" % j], T["pks%d" % i][:], [T["lns%d" % j][:]]))
-        if dq == N - 1:
-            wait("p", [ps])
-            send(pls)
+        of, nq = T["of%d" % i], nio(q)
+        wd = 168 if nq == 11 else 160
+        if n == 0: y = [V("copy", [io], block(of, k, q), block(T.iof, q, q)) for k in range(4)][-1]
+        else: y = V("copy", [z], of[:, 0:nq], T["sp%d" % i][:, 0:nq])
+        z = spread(to[n + 1], T["sp%d" % at(to[n + 1], r)]) if n < 2 else None
+        off = of[:, 0:nq]
+        pq = V("copy", [y, hal, qz], U32(T["pkq%d" % i][:, 0:16 * nq]), U32(T.winq[:]).indirect(off))
+        pss.append(S("act", [y, hal, qz], T["pks%d" % i][:, 0:16 * nq], T.wins[:].indirect(off), F.Copy))
+        pls.append(([q], eng[q][4 * n:4 * n + 4], T.sem["cs%d" % j], T["pks%d" % i][:, 0:wd], [T.es[:, RG * r:RG * r + wd]]))
         wait("p", [pq])
-        send([([q], eng[q], T.sem["cq%d" % j], U8(T["pkq%d" % i][:]), [U8(T["lnq%d" % j][:])])])
-    fill(8)
-    x = V("tt", [tk["gq"]], T.bq[:, 0:8], T.slot[:], T.gq[:, 0:8], A.add)
-    y = V("tt", [], T.bq[:, 8:16], T.gq[:, 8:16], T.gq[:, 16:24], A.add)
-    pe = [V("copy", [tk["own"]], U32(T.eq[:, 160 * r:160 * r + 160]), U32(T.winq[:]).indirect(T.ioo[:]))]
-    pf = [S("act", [tk["own"]], T.es[:, 160 * r:160 * r + 160], T.wins[:].indirect(T.ioo[:]), F.Copy)]
-    x = V("tt", [y], T.bq[:, 16:24], T.bq[:, 0:8], T.bq[:, 8:16], A.add)
-    V("quant", [ldw[1]], T.wq[:, W(1)], T.ws[:, W(1)], T.wt[:, W4(1)])
-    x = V("tt", [x], T.bq[:, 24:32], T.bq[:, 16:24], T.gq[:, 24:32], A.max)
-    ix = ("idx", 3 * ne)
-    fo = lambda k: V("ts", [x], T.fo[:, 8 * k:8 * k + 8], T.bq[:, 24:32], 32.0 * k, None, A.add)
-    for k in range(4):
-        z = V("copy", [ix], T.lb[32 * k:32 * k + 32, 0:15], T.li[32 * r:32 * r + 32, 0:15])
-    fo(0)
-    fo(1)
-    z = V("copy", [z], T.lbi[:, 0:15], T.lb[:, 0:15])
-    fo(2)
-    fo(3)
-    V("ts", [z], T.llo[:, 0:15], T.lbi[:, 0:15], 255, None, A.bitwise_and)
-    z = V("ts", [], T.lhi[:, 0:15], T.lbi[:, 0:15], 8, None, A.logical_shift_right)
-    fd = fo(4)
-    V("copy", [z], T.lo[:, 0:30:2], T.llo[:, 0:15])
-    z = V("copy", [], T.lo[:, 1:30:2], T.lhi[:, 0:15])
+        send([([q], eng[q], T.sem["cq%d" % j], U8(T["pkq%d" % i][:, 0:wd]), [U8(T.eq[:, RG * r:RG * r + wd])])])
+        if r == 0 and n == 1:
+            wait("p", pss[:1])
+            send(pls[:1])
+    wait("p", pss[2:])
+    send(pls[1:] if r == 0 else pls)
+    x = V("tt", [en], T.en[:, 4:6], T.en[:, 0:2], T.inf[:, 8:17:8], A.add) if ex_out else None
+    z = spread(r, T.spo)
+    x = V("ts", [x], T.nen[:], T.en[:], -1.0, -0.5, A.mult, A.add)
+    G = lambda c: T.g[:, 8 * c:8 * c + 8]
+    for c in (2, 3, 0, 1, 4, 5):
+        x = S("sign", [x], G(c), T.nP[:], T.nen[:, c:c + 1])
+    no = nio(r)
+    y = V("copy", [z], T.ioo[:, 0:no], T.spo[:, 0:no])
+    off = T.ioo[:, 0:no]
+    pe = V("copy", [y], U32(T.eq[:, RG * r:RG * r + 16 * no]), U32(T.winq[:]).indirect(off))
+    pf = S("act", [y], T.es[:, RG * r:RG * r + 16 * no], T.wins[:].indirect(off), F.Copy)
+    y = V("tt", [x], T.gb[:], G(2), G(3), A.add)
+    V("tt", [], T.ga[:], G(0), G(1), A.add)
+    b = V("tt", [], T.gc1[:], G(4), G(5), A.add)
+    x = V("tt", [y], T.gs[:], T.gb[:], T.slot[:], A.add)
+    b = V("tt", [b], T.bb[:], T.ga[:], T.gc1[:], A.subtract) if r < 2 else V("tt", [], T.bb[:], G(1), G(5), A.subtract)
+    y = V("tt", [x], T.b0[:], T.ga[:], T.gs[:], A.add)
+    b = V("tt", [b], T.uu[:], T.bb[:], T.cE[:], A.mult)
+    x = V("tt", [], T.b1[:], T.gc1[:], T.gs[:], A.add)
+    V("ts", [y], T.fo[:], T.b0[:], RG / 2.0, None, A.mult)
+    b = V("tt", [b, x], T.b2[:], T.b1[:], T.uu[:], A.add)
+    fd = V("ts", [b], T.fu[:], T.b2[:], RG / 2.0, None, A.mult)
     qw = V("quant", [ldw[2]], T.wq[:, W(2)], T.ws[:, W(2)], T.wt[:, W4(2)])
-    for dq in range(1, N):
-        q = (r - dq) % N
-        i = at(q, r)
-        off = T.lo[:, 10 * i:10 * i + 10]
-        pe.append(V("copy", [z, ("cq%d" % i, ne)], U32(T.eq[:, 160 * q:160 * q + 160]), U32(T["lnq%d" % i][:]).indirect(off)))
-        pf.append(S("act", [z, ("cs%d" % i, 4)], T.es[:, 160 * q:160 * q + 160], T["lns%d" % i][:].indirect(off), F.Copy))
 
-    for k in range(5):
-        lo, hi = 128 * k, 128 * k + 128
-        a = V("copy", [pe[-1], fd], U32(T.xfq[:, lo:hi]), U32(T.eq[:]).indirect(T.fo[:, 8 * k:8 * k + 8]))
-        b = S("act", [pf[-1], fd], T.xfs[:, lo:hi], T.es[:].indirect(T.fo[:, 8 * k:8 * k + 8]), F.Copy)
+    cq = [("cq%d" % i, ne) for i in (2, 1, 0)]
+    cs = [("cs%d" % i, 4) for i in (2, 1, 0)]
+    for n, k in enumerate((0, 1, 2, 4, 3)):
+        lo, hi = 128 * n, 128 * n + 128
+        s = slice(32 * k, 32 * k + 4 * RG + 32)
+        off = (T.fu if k == 3 else T.fo)[:]
+        a = V("copy", [pe, fd] + cq, U32(T.xfq[:, lo:hi]), U32(T.eq[:, s]).indirect(off))
+        b = S("act", [pf, fd, ze] + cs, T.xfs[:, lo:hi], T.es[:, s].indirect(off), F.Copy)
         ms = []
         for o in range(2):
-            w = 128 * (2 * k + o)
+            w = 128 * (2 * KPOS[k] + o)
             ms.append(op("t", "mm", [a, b, qw], T.yp[:, 512 * o:512 * o + 128], T.wq[:, w:w + 128], T.ws[:, w:w + 128],
-                         T.xfq[:, lo:hi], T.xfs[:, lo:hi], k == 0, k == 4))
+                         T.xfq[:, lo:hi], T.xfs[:, lo:hi], n == 0, n == 4))
     x = V("copy", [ms[0]], T.ys[:, 0:128], T.yp[:, 0:128])
     dma("s", "st0", [x], T.y[:, 0:128], T.ys[:, 0:128])
     x = S("act", [ms[1]], T.ys[:, 128:256], T.yp[:, 512:640], F.Copy)
     dma("a", "st1", [x], T.y[:, 128:256], T.ys[:, 128:256])
     wait("p", [(k, n) for k, n in cnt.items()])
-    wait("p", [hal, inf, ix])
+    wait("p", [hal, inf, bdr, flg])

@@ -1,13 +1,11 @@
 from concourse.bass import DstId, RemoteDMATransfer
-from concourse.mybir import dt, AluOpType, ActivationFunctionType, AxisListType
+from concourse.mybir import dt, AluOpType, ActivationFunctionType
 
 A = AluOpType
 F = ActivationFunctionType
 CODE = "float8_e4m3fn_x4"
-X0 = 128
-ZC = 448
 RG = 176
-KPOS = [3, 0, 4, 1, 2]
+U = 1.0 / 128
 
 
 def sb(n, d="float32"): return ("sbuf", [128, n], d)
@@ -15,33 +13,33 @@ def sb(n, d="float32"): return ("sbuf", [128, n], d)
 
 BF, I32, U16 = "bfloat16", "int32", "uint16"
 SCRATCH = {
-    "ut": sb(512, BF), "xt": sb(1024, BF), "wt": sb(5120, BF), "zt": sb(640, BF),
+    "ut": sb(512, BF), "xt": sb(1024, BF), "wt": sb(5120, BF), "zt": sb(640, BF), "xp": sb(1216, BF),
     "uq": sb(128, CODE), "us": sb(128, "uint8"), "urq": sb(128, CODE), "urs": sb(128, "uint8"),
-    "winq": sb(544, CODE), "wins": sb(544, "uint8"),
+    "xq": sb(256, CODE), "xs": sb(256, "uint8"), "padq": sb(544, CODE), "pads": sb(544, "uint8"),
     "wq": sb(1280, CODE), "ws": sb(1280, "uint8"),
     "eq": sb(4 * RG + 160, CODE), "es": sb(4 * RG + 160, "uint8"),
     "xfq": sb(640, CODE), "xfs": sb(640, "uint8"),
     "off0": sb(8, U16), "ys": sb(256),
-    "sc": ("psum", [128, 512], "float32"), "yp": ("psum", [128, 1024], "float32"),
-    "pI": sb(1, I32), "pm": sb(4, I32), "p16": sb(1), "a8": sb(1), "bc": sb(4), "bE": sb(1), "x8": sb(1),
-    "i64": sb(8), "i16": sb(8), "tgt": sb(2), "nP": sb(8), "slot": sb(8), "cE": sb(8), "kk": sb(8),
-    "half": sb(256, BF), "zb": sb(256, BF), "two": sb(16, BF), "ip": sb(16),
+    "sc": ("psum", [128, 1024], "float32"), "yp": ("psum", [128, 1024], "float32"),
+    "pI": sb(1, I32), "pm": sb(4, I32), "pf": sb(4), "i64": sb(8), "i16": sb(8), "kk": sb(8), "kv": sb(8),
+    "b2": sb(1), "b3": sb(1), "nb3": sb(1), "nb2": sb(1), "b7": sb(1), "p16": sb(1), "x8": sb(1),
+    "tp": sb(2), "tp5": sb(2), "te": sb(1), "nP": sb(8), "slot": sb(8), "cE": sb(8), "half": sb(256, BF), "zb": sb(288, BF),
+    "B": sb(64, BF), "BT": sb(64, BF), "EL": sb(64, BF), "eb": sb(64, BF),
     "P": sb(256, BF), "n2": sb(256, BF), "hp": sb(288, BF), "vp": sb(256, BF), "vn": sb(272, BF), "m1": sb(256, BF), "gh": sb(256, BF),
-    "v2": sb(256, BF), "o2": sb(256, BF), "l": sb(272, BF), "S": sb(272, BF), "ob": sb(32, BF), "e": sb(32, BF),
-    "pk": sb(48), "bd": sb(16), "ub": sb(32, I32), "u2": sb(32, I32), "fb": sb(16, I32), "f2": sb(16, I32),
-    "inf": sb(32, BF), "en": sb(6), "nen": sb(6), "tI": sb(2, I32), "tJ": sb(2, I32), "tb": sb(2),
-    "junk": sb(544, BF), "acl": sb(2), "cI": sb(2, I32), "jI": sb(2, I32), "cf": sb(6), "iof": sb(12),
-    "eI": sb(1, I32), "eJ": sb(1, I32), "eT": sb(1), "eB": sb(16), "eR": sb(1),
-    "g": sb(48), "ga": sb(8), "gb": sb(8), "gc1": sb(8), "gs": sb(8), "b0": sb(8), "b1": sb(8), "bb": sb(8), "uu": sb(8), "b2": sb(8),
-    "fo": sb(8, U16), "fu": sb(8, U16), "ioo": sb(12, U16), "spo": sb(12),
+    "v2": sb(256, BF), "o2": sb(256, BF), "l": sb(256, BF), "S": sb(288, BF), "FT": sb(32, BF), "RB": sb(32, BF), "R16": sb(32, BF), "Sl": sb(16, BF),
+    "bd": sb(16, BF), "inf": sb(32, BF), "r0": sb(32, BF), "fl": sb(8, BF),
+    "D": sb(2), "D0": sb(2), "D5": sb(2), "K": sb(2, I32), "tb": sb(2), "E1": sb(1), "E5": sb(1), "De": sb(1), "Ke": sb(1, I32), "tbe": sb(1),
+    "junk": sb(288, BF), "junk2": sb(288, BF), "junk3": sb(288, BF), "junk4": sb(16, BF), "acl": sb(2), "ace": sb(1), "iof": sb(12),
+    "en": sb(6), "g": sb(48), "gac": sb(16), "gb": sb(8), "gs": sb(8), "b1": sb(8), "bb": sb(8), "uu": sb(8), "bf": sb(16),
+    "fo": sb(16, U16), "ioo": sb(12, U16), "spo": sb(12),
 }
 for _i in range(3):
     SCRATCH["of%d" % _i] = sb(12, U16)
     SCRATCH["sp%d" % _i] = sb(12)
     SCRATCH["pkq%d" % _i] = sb(RG, CODE)
     SCRATCH["pks%d" % _i] = sb(RG, "uint8")
-SEMAPHORES = ["vc", "ac", "tc", "pc", "ldu", "ldx", "ldw0", "ldw1", "ldw2", "halo", "bdr", "info", "flg",
-              "cq0", "cq1", "cq2", "cs0", "cs1", "cs2", "sent", "st0", "st1"]
+SEMAPHORES = ["vc", "ac", "tc", "pc", "ldu", "ldxa", "ldxb", "ldw0", "ldw1", "ldw2", "ldw3", "ldw4", "halo", "bdr", "inf0", "inf1", "inf2", "inf3",
+              "r0s", "flg", "cq0", "cq1", "cq2", "cs0", "cs1", "cs2", "sent", "st0", "st1"]
 
 
 def rank_program(g, core, T, topo):
@@ -71,12 +69,13 @@ def rank_program(g, core, T, topo):
         elif name == "tt": i = q.tensor_tensor(*args)
         elif name == "ts": i = q.tensor_scalar(*args)
         elif name == "copy": i = q.tensor_copy(*args)
-        elif name == "red": i = q.tensor_reduce(args[0], args[1], AxisListType.X, A.add)
         elif name == "scan": i = q.tensor_tensor_scan(*args)
+        elif name == "turn": i = q.transpose(*args)
         elif name == "quant": i = q.quantize_mx(*args)
         elif name == "act": i = q.activation(*args)
-        elif name == "sign": i = q.activation(args[0], args[1], F.Sign, bias=args[2], scale=1.0)
-        elif name == "sum": i = q.activation(args[0], args[1], F.Sign, bias=args[2], scale=1.0, accum_out=args[3])
+        elif name == "lin": i = q.activation(args[0], args[1], F.Identity, bias=args[3], scale=args[2])
+        elif name == "sign": i = q.activation(args[0], args[1], F.Sign, bias=args[3], scale=args[2])
+        elif name == "sum": i = q.activation(args[0], args[1], F.Sign, bias=args[3], scale=args[2], accum_out=args[4])
         elif name == "mm": i = q.matmul_mx(*args)
         elif name == "iota": i = q.iota(*args)
         else: i = q.iota(*args, allow_small_or_imprecise_dtypes=True)
@@ -105,221 +104,243 @@ def rank_program(g, core, T, topo):
     def at(q, me): return q if q < me else q - 1
     eng = {q: topo.engines(core, T.cores[q]) for q in others}
     ne = min(len(eng[q]) for q in others)
-    W = lambda k: slice(512 * k, min(1280, 512 * k + 512))
-    W4 = lambda k: slice(2048 * k, min(5120, 2048 * k + 2048))
+    e0 = eng[others[0]]
+    h2 = ne // 2
 
     up, dn = r > 0, r < N - 1
-    ex_out = r in (0, 1)
-    L = 272 if r == 0 else 256
+    ex_out, ex_in = r in (0, 1), r in (1, 2)
+    PB = 128 if dn else 129
+    L = 288 if r == 0 else 272
     ldu = dma("a", "ldu", [], T.ut[:, 0:8], T.u[:, 0:8])
-    ldx = dma("s", "ldx", [], T.xt[:], T.x[:])
-    mu = V("memset", [], T.ut[:, 8:512], 0.0)
-    mo = V("memset", [], T.off0[:], 0)
+    h0, h1 = (0, 1) if up else (1, 0)
+    X = lambda h: slice(512 * h, 512 * h + 512)
+    ldxa = dma("s", "ldxa", [], T.xt[:, X(h0)], T.x[:, X(h0)])
+    ldxb = dma("a", "ldxb", [], T.xt[:, X(h1)], T.x[:, X(h1)])
     kp = op("p", "iota", [], T.pI[:], [[0, 1]], 0, 1)
     op("p", "iotaf", [], T.i64[:], [[64, 8]], 0, 0)
     op("p", "iotaf", [], T.i16[:], [[0, 4], [16, 2]], 0, 0)
-    op("p", "iotaf", [], T.kk[:, 0:3], [[-2, 3]], -2 * (X0 - 1) - L, 0)
-    kg = op("p", "iotaf", [], T.kk[:, 3:5], [[-64, 2]], -2 * (X0 - 16) - L, 0)
-    V("memset", [], T.zb[:], 0.0)
-    V("memset", [], T.vn[:, 0:16], -3.0)
-    V("memset", [], T.vn[:, 256:272], -3.0)
-    V("memset", [], T.half[:], 0.5)
-    V("memset", [], T.cf[:, 2:4], 0.0)
-    k2 = V("memset", [], T.two[:], 2.0)
-    mz = V("memset", [], T.zt[:], 0.0)
+    op("p", "iotaf", [], T.kk[:, 0:3], [[-2, 3]], -2 * (PB - 1) - L, 0)
+    op("p", "iotaf", [], T.kk[:, 3:5], [[-68, 2]], -2 * (PB - 17) - L, 0)
+    op("p", "iotaf", [], T.kv[:, 0:3], [[1, 3]], PB - 1 + 128, 0)
+    kg = op("p", "iotaf", [], T.kv[:, 3:5], [[34, 2]], PB - 17 + 128, 0)
+    mu = V("memset", [], T.ut[:, 8:512], 0.0)
+    mo = V("memset", [], T.off0[:], 0)
     V("ts", [kp], T.pm[:, 3:4], T.pI[:], 5, None, A.logical_shift_right)
     V("ts", [], T.pm[:, 0:1], T.pI[:], 15, None, A.bitwise_and)
     V("ts", [], T.pm[:, 1:2], T.pI[:], 7, None, A.bitwise_and)
-    kc = V("ts", [], T.pm[:, 2:3], T.pI[:], 3, 1, A.logical_shift_right, A.bitwise_and)
+    k = V("ts", [], T.pm[:, 2:3], T.pI[:], 3, 1, A.logical_shift_right, A.bitwise_and)
+    mB = V("memset", [], T.B[:], 0.0)
+    kf = V("copy", [k], T.pf[:], T.pm[:])
+    mz = V("memset", [], T.zt[:], 0.0)
 
     qu = V("quant", [ldu, mu], T.uq[:], T.us[:], T.ut[:])
     pu = V("copy", [qu, mo], U32(T.urq[:]), U32(T.uq[:]).indirect(T.off0[:]))
     pv = S("act", [qu, mo], T.urs[:], T.us[:].indirect(T.off0[:]), F.Copy)
-    qx = V("quant", [ldx], T.winq[:, X0:X0 + 256], T.wins[:, X0:X0 + 256], T.xt[:])
-    mm = op("t", "mm", [pu, pv, qx], T.sc[:, 0:256], T.urq[:], T.urs[:], T.winq[:, X0:X0 + 256], T.wins[:, X0:X0 + 256], True, True)
-    ldw = [dma("s", "ldw0", [ldx], T.wt[:, W4(0)], T.w[:, W4(0)])]
+    qx, mm = {}, {}
 
-    nb = ([(r - 1, X0, X0 + 256)] if up else []) + ([(r + 1, X0 + 240, X0 - 16)] if r == N - 2 else [])
+    def score(h, ld):
+        c = slice(128 * h, 128 * h + 128)
+        qx[h] = V("quant", [ld], T.xq[:, c], T.xs[:, c], T.xt[:, X(h)])
+        mm[h] = op("t", "mm", [pu, pv, qx[h]], T.sc[:, 512 * h:512 * h + 128], T.urq[:], T.urs[:], T.xq[:, c], T.xs[:, c], True, True)
+    score(h0, ldxa)
+    V("memset", [], T.half[:], 0.5)
+    V("memset", [], T.vn[:, 0:16], -3.0)
+    V("memset", [], T.vn[:, 256:272], -3.0)
+    kz = V("memset", [], T.zb[:], 0.0)
+    score(h1, ldxb)
+    ldw, qw = {}, {}
 
-    def strips(view):
+    def load_w(k, deps): ldw[k] = dma("s", "ldw%d" % k, deps, T.wt[:, 1024 * k:1024 * k + 1024], T.w[:, 1024 * k:1024 * k + 1024])
+    def quant_w(k): qw[k] = V("quant", [ldw[k]], T.wq[:, 256 * k:256 * k + 256], T.ws[:, 256 * k:256 * k + 256], T.wt[:, 1024 * k:1024 * k + 1024])
+    load_w(4, [ldxb])
+
+    nb = ([(r - 1, 0, 400)] if up else []) + ([(r + 1, 240, 112)] if r == N - 2 else [])
+
+    def strips(view, nb):
         if nb:
-            send([([q], eng[q][k * (ne // 2):(k + 1) * (ne // 2)], T.sem.halo, view(src, src + 16), [view(dst, dst + 16)])
-                  for k, (q, src, dst) in enumerate(nb)])
-    wait("p", [qx])
-    strips(lambda a, b: U8(T.winq[:, a:b]))
-    hal = ("halo", 2 * (ne // 2))
+            send([([q], eng[q][(src > 0) * h2:(src > 0) * h2 + h2], T.sem.halo, view("xq", "xs", src), [view("padq", "pads", dst)]) for q, src, dst in nb])
+    for b in nb:
+        wait("p", [qx[b[1] > 0]])
+        strips(lambda q, s, a: U8(T[q][:, a:a + 16]), [b])
+    hal = ("halo", 2 * h2)
 
-    kip = V("scan", [k2], T.ip[:], T.two[:], T.zb[:, 0:16], 2.0 ** -16, A.mult, A.add)
-    V("ts", [kc], T.bc[:, 0:1], T.pm[:, 2:3], 32.0, None, A.mult)
-    k = V("copy", [kc], T.bc[:, 1:2], T.pm[:, 1:2])
-    V("ts", [kc], T.p16[:], T.pm[:, 0:1], 2.0 / RG, 4 + 0.5 / RG, A.mult, A.add)
-    V("ts", [kc], T.a8[:], T.pm[:, 3:4], 8.0, None, A.mult)
-    V("ts", [kc], T.x8[:], T.pm[:, 2:3], -8.0 / RG, 64.0 / RG, A.mult, A.add)
+    S("lin", [kf, kg], T.b2[:], T.pf[:, 2:3], 32.0, T.pf[:, 1:2])
+    k = S("lin", [], T.p16[:], T.pf[:, 0:1], 2.0 / RG, 4 + 0.5 / RG)
+    k = S("lin", [k], T.b3[:], T.pf[:, 3:4], 8.0, T.b2[:])
+    k = S("lin", [k], T.nb3[:], T.b3[:], -U, -0.5 * U)
+    S("lin", [], T.x8[:], T.pf[:, 2:3], -8.0 / RG, 64.0 / RG)
+    k = S("lin", [k], T.tp[:], T.i64[:, 0:2], -U, T.nb3[:])
+    S("lin", [], T.b7[:], T.pf[:, 3:4], 8.0, T.pf[:, 1:2])
+    k = S("lin", [k], T.tp5[:], T.tp[:], 1.0, 0.5)
+    S("lin", [], T.nb2[:], T.b2[:], U, 8.0 * r * U)
+    S("lin", [k], T.te[:], T.b7[:], -1.0 / 32, -0.5 / 32)
+    k = S("lin", [], T.slot[:], T.i16[:], 2.0 / RG, T.p16[:])
+    S("lin", [k], T.nP[:], T.i64[:], U, T.nb2[:])
+    kS = S("lin", [], T.cE[:], T.i16[:], -1.0 / RG, T.x8[:])
+    xp0 = 128 if dn else 4
+    for i in range(16): kX = S("act", [ldxa, ldxb], T.xp[:, xp0 + 68 * i:xp0 + 68 * i + 64], T.xt[:, 64 * i:64 * i + 64], F.Copy)
 
-    if up: V("ts", [mm], T.P[:, 0:16], T.sc[:, 0:16], 0.0, None, A.is_gt)
-    if dn: V("ts", [mm], T.P[:, 240:256], T.sc[:, 240:256], 0.0, None, A.is_gt)
-    a, b = (16 if up else 0), (240 if dn else 256)
-    kr = ("vc", cnt["vc"])
-    p = V("ts", [mm], T.P[:, a:b], T.sc[:, a:b], 0.0, None, A.is_gt)
-    if up: ka = V("scan", [kr], T.pk[:, 0:16], T.two[:], T.P[:, 0:16], 2.0 ** -17, A.mult, A.add)
-    if dn: ka = V("scan", [kr], T.pk[:, 16:32], T.two[:], T.P[:, 240:256], 2.0 ** -17, A.mult, A.add)
+    if up: kb = V("ts", [mm[0], mB], T.B[:, 32:48], T.sc[:, 0:16], 0.0, None, A.is_gt)
+    if dn: kb = V("ts", [mm[1], mB], T.B[:, 0:16], T.sc[:, 624:640], 0.0, None, A.is_gt)
+    kb = V("turn", [kb], T.BT[:], T.B[:])
+    for h in (h0, h1): p = V("ts", [mm[h]], T.P[:, 128 * h:128 * h + 128], T.sc[:, 512 * h:512 * h + 128], 0.0, None, A.is_gt)
+    wait("p", [kb])
+    send(([([r - 1], eng[r - 1][:h2], T.sem.bdr, T.BT[:, 32:33], [T.bd[:, 8:9]])] if up else [])
+         + ([([r + 1], eng[r + 1][h2:], T.sem.bdr, T.BT[:, 0:1], [T.bd[:, 0:1]])] if dn else []))
+    strips(lambda q, s, a: T[s][:, a:a + 16], nb)
     n2 = V("ts", [p], T.n2[:], T.P[:], -2.0, None, A.add)
-    wait("p", [ka])
-    send(([([r - 1], eng[r - 1][:ne // 2], T.sem.bdr, T.pk[:, 15:16], [T.bd[:, 4:5]])] if up else [])
-         + ([([r + 1], eng[r + 1][ne // 2:], T.sem.bdr, T.pk[:, 31:32], [T.bd[:, 0:1]])] if dn else []))
-    strips(lambda a, b: T.wins[:, a:b])
-    h = V("scan", [n2], T.hp[:, 16:271], T.P[:, 0:255], T.n2[:, 1:256], -100.0, A.max, A.add)
+    h = V("scan", [n2, kz], T.hp[:, 16:271], T.P[:, 0:255], T.n2[:, 1:256], -100.0, A.max, A.add)
     v = V("scan", [], T.vp[:, 0:240], T.P[:, 0:240], T.n2[:, 16:256], -100.0, A.max, A.add)
     h = V("memset", [h], T.hp[:, 31:272:16], 0.0)
     v = V("ts", [v], T.vn[:, 16:256], T.vp[:, 0:240], -1.0, -3.0, A.is_equal, A.add)
     h = V("ts", [h], T.m1[:], T.hp[:, 16:272], -1.0, None, A.is_equal)
     v = V("scan", [v], T.v2[:], T.vn[:, 16:272], T.vn[:, 0:256], -100.0, A.max, A.add)
     h = V("scan", [h], T.gh[:], T.half[:], T.m1[:], 0.0, A.mult, A.max)
-    if up: V("copy", [], T.ob[:, 0:16], T.P[:, 0:16])
+    V("memset", [], T.xp[:, 0:128] if dn else T.xp[:, 1088:1216], 0.0)
     h = V("scan", [h, v], T.o2[:], T.gh[:], T.v2[:], -100.0, A.max, A.add)
-    if dn: V("copy", [], T.ob[:, 16:32], T.P[:, 240:256])
-    l = V("ts", [h], T.l[:, 0:256], T.o2[:], -5.6, None, A.is_gt)
-    ldw.append(dma("s", "ldw1", [h], T.wt[:, W4(1)], T.w[:, W4(1)]))
+    load_w(0, [h])
+    l = V("ts", [h], T.l[:], T.o2[:], -5.6, U, A.is_gt, A.mult)
+    for t in range(4): mp = V("memset", [], T.xp[:, (192 if dn else 0) + t:1216 if dn else 1088:68], 0.0)
 
-    k = V("tt", [k], T.bc[:, 2:3], T.bc[:, 0:1], T.bc[:, 1:2], A.add)
-    V("ts", [kg], T.slot[:], T.i16[:], 2.0 / RG, T.p16[:], A.mult, A.add)
-    V("ts", [], T.cE[:], T.i16[:], -1.0 / RG, T.x8[:], A.mult, A.add)
-    k = V("tt", [k], T.bc[:, 3:4], T.bc[:, 2:3], T.a8[:], A.add)
-    V("ts", [], T.nP[:], T.i64[:], T.bc[:, 2:3], 8.0 * r, A.add, A.add)
-    kt = V("ts", [k], T.tgt[:], T.i64[:, 0:2], T.bc[:, 3:4], 1023.0, A.add, A.add)
-    if ex_out: V("ts", [], T.bE[:], T.a8[:], T.bc[:, 1:2], 1023.0, A.add, A.add)
-    for a in ([0, 400] if dn else [384]):
-        qz = V("quant", [mz], T.winq[:, a:a + 128], T.wins[:, a:a + 128], T.zt[:, 0:512])
+    bdr = ("bdr", h2 * len([q for q in (r - 1, r + 1) if 0 <= q < N]))
+    a, b = (0 if up else 32), (64 if dn else 32)
+    if up: x = V("ts", [bdr], T.EL[:, 0:32], T.BT[:, 32:64], T.bd[:, 0:1], U, A.not_equal, A.mult)
+    if dn: x = V("ts", [bdr], T.EL[:, 32:64], T.BT[:, 0:32], T.bd[:, 8:9], U, A.not_equal, A.mult)
+    x = V("turn", [x], T.eb[:, a:b], T.EL[:, a:b])
+    if up: l = V("tt", [x, l], T.l[:, 0:16], T.l[:, 0:16], T.eb[:, 0:16], A.max)
+    if dn: l = V("tt", [x, l], T.l[:, 240:256], T.l[:, 240:256], T.eb[:, 32:48], A.max)
+    sS = V("scan", [l], T.S[:, 0:256], T.l[:], T.zb[:, 0:256], 0.0, A.add, A.add)
+    if ex_in: ft = V("turn", [], T.FT[:], T.l[:, 0:32])
+    wait("p", [sS])
+    down = others[::-1]
+    send([(down, e0, T.sem["inf%d" % r], T.S[:, 255:256], [T.inf[:, 8 * r:8 * r + 1]] * 3)])
+    if ex_in:
+        wait("p", [ft])
+        send([([r - 1], e0[h2:], T.sem.flg, T.FT[:, 0:1], [T.fl[:, 0:1]]),
+              (down, e0[:h2], T.sem.r0s, T.S[:, 15:16], [T.r0[:, 8 * r:8 * r + 1]] * 3)])
+    inf = [("inf%d" % q, ne) for q in range(N)]
+    r0s = ("r0s", h2 * (1 if ex_in else 2))
+    flg = ("flg", h2) if ex_out else None
 
-    n0 = T.en[:, r - 1:r] if up else -1.0
-    mine = [lambda d: V("ts", [d], T.tI[:], T.tgt[:], n0, None, A.subtract),
-            lambda d: V("ts", [d], T.tJ[:], T.tI[:], 127, None, A.bitwise_and),
-            lambda d: V("ts", [d], T.tb[:], T.tJ[:], -1.0, -0.5, A.mult, A.add)]
-    if r == 0:
-        m = kt
-        for f in mine: m = f(m)
+    sp = V("copy", [sS], T.S[:, 256:272], T.S[:, 15:256:16])
+    own = V("copy", [], T.inf[:, 8 * r:8 * r + 1], T.S[:, 255:256])
+    if ex_in: own = V("copy", [], T.r0[:, 8 * r:8 * r + 1], T.S[:, 15:16])
+    if ex_out: E1 = V("ts", [kS], T.E1[:], T.S[:, 255:256], 4.0, T.te[:], A.mult, A.add)
+    if dn: V("quant", [mz], T.padq[:, 416:544], T.pads[:, 416:544], T.zt[:, 0:512])
+    if ex_out: V("ts", [E1], T.E5[:], T.E1[:], 0.5, None, A.add)
+    a = 96 if dn else 128
+    pp = V("quant", [kX, mp], T.padq[:, a:a + 304], T.pads[:, a:a + 304], T.xp[:])
+    for k in (1, 2, 3): load_w(k, [pp])
+    quant_w(4)
 
-    bdr = ("bdr", (ne // 2) * len([q for q in (r - 1, r + 1) if 0 <= q < N]))
-    a, b = (0 if up else 16), (32 if dn else 16)
-    if up: x = V("ts", [bdr, kip], T.ub[:, 0:16], T.ip[:], T.bd[:, 0:1], -0.5, A.mult, A.add)
-    if dn: x = V("ts", [bdr, kip], T.ub[:, 16:32], T.ip[:], T.bd[:, 4:5], -0.5, A.mult, A.add)
-    x = V("ts", [x], T.u2[:, a:b], T.ub[:, a:b], 1, None, A.bitwise_and)
-    x = V("tt", [x], T.e[:, a:b], T.u2[:, a:b], T.ob[:, a:b], A.not_equal)
-    if up: l = V("tt", [x], T.l[:, 0:16], T.l[:, 0:16], T.e[:, 0:16], A.max)
-    if dn: l = V("tt", [x], T.l[:, 240:256], T.l[:, 240:256], T.e[:, 16:32], A.max)
-    sS = V("scan", [l], T.S[:, 0:256], T.l[:, 0:256], T.zb[:], 0.0, A.add, A.add)
-    if r in (1, 2): V("scan", [], T.pk[:, 32:48], T.two[:], T.l[:, 0:16], 2.0 ** -17, A.mult, A.add)
-    t = V("copy", [sS], T.inf[:, 8 * r:8 * r + 2], T.S[:, 15:256:240])
-    wait("p", [t])
-    e0 = eng[others[0]]
-    nB = lambda q: ne // 2 if q in (1, 2) else ne
-    send([(others, e0[:nB(r)], T.sem.info, T.inf[:, 8 * r:8 * r + 2], [T.inf[:, 8 * r:8 * r + 2]] * 3)]
-         + ([([r - 1], e0[ne // 2:], T.sem.flg, T.pk[:, 47:48], [T.bd[:, 8:9]])] if r in (1, 2) else []))
-    inf = ("info", sum(nB(q) for q in others))
-    flg = ("flg", ne // 2) if ex_out else None
-    ldw.append(dma("s", "ldw2", [t], T.wt[:, W4(2)], T.w[:, W4(2)]))
-    ze = V("quant", [], T.eq[:, 4 * RG:4 * RG + 160], T.es[:, 4 * RG:4 * RG + 160], T.zt[:])
-    for c in (0, 1): V("quant", [ldw[c]], T.wq[:, W(c)], T.ws[:, W(c)], T.wt[:, W4(c)])
-
-    def ends(d): return V("scan", [inf, t], T.en[:, 0:4], T.inf[:, 1:32:8], T.zb[:, 0:4], -1.0, A.add, A.add)
-
-    row16 = [lambda d: V("ts", [flg], T.fb[:], T.ip[:], T.bd[:, 8:9], -0.5, A.mult, A.add),
-             lambda d: V("ts", [d], T.f2[:], T.fb[:], 1, None, A.bitwise_and),
-             lambda d: V("copy", [d], T.l[:, 256:272], T.f2[:]),
-             lambda d: V("scan", [d], T.S[:, 256:272], T.l[:, 256:272], T.zb[:, 0:16], T.S[:, 255:256], A.add, A.add)]
-    if r == 0:
-        x = None
-        for f in row16: x = f(x)
-        sS = x
+    if r == 0: tb, m = T.tp, kS
     else:
-        x = m = None
-        for i, f in enumerate([ends] + mine):
-            if r == 1 and i: x = row16[i - 1](x)
-            m = f(m)
-            if i == 0: en = m
-    for c in range(2):
-        al = S("sum", [sS, m], T.junk[:, 272 * c:272 * c + L], T.S[:, 0:L], T.tb[:, c:c + 1], T.acl[:, c:c + 1])
-    if r == 0: en = ends(None)
-    if r == 1: x = row16[3](x)
+        tb = T.tb
+        i0, i1, i2 = T.inf[:, 0:1], T.inf[:, 8:9], T.inf[:, 16:17]
+        if r == 1:
+            V("ts", [kS, inf[0]], T.D[:], T.tp[:], i0, None, A.add)
+            x = V("ts", [], T.K[:], T.tp5[:], i0, None, A.add)
+            V("ts", [], T.De[:], i0, 4.0, T.E1[:], A.mult, A.add)
+        else:
+            a, b = (T.D, T.K) if r == 2 else (T.D0, T.D5)
+            V("ts", [kS, inf[0], inf[1]], a[:], T.tp[:], i0, i1, A.add, A.add)
+            x = V("ts", [], b[:], T.tp5[:], i0, i1, A.add, A.add)
+            if r == 3:
+                V("ts", [x, inf[2]], T.D[:], T.D0[:], i2, None, A.add)
+                x = V("ts", [], T.K[:], T.D5[:], i2, None, A.add)
+        m = V("tt", [x], T.tb[:], T.D[:], T.K[:], A.subtract)
+        if r == 1: k = V("ts", [], T.Ke[:], i0, 4.0, T.E5[:], A.mult, A.add)
+    if r == 0:
+        k = V("ts", [], T.Ke[:], T.E1[:], 0.5, None, A.add)
+        x = V("ts", [flg, kz], T.RB[:], T.zb[:, 0:32], T.fl[:, 0:1], None, A.add)
+        k = V("tt", [k], T.tbe[:], T.E1[:], T.Ke[:], A.subtract)
+        x = V("turn", [x], T.R16[:], T.RB[:])
+        sp = V("scan", [x], T.S[:, 272:288], T.R16[:, 0:16], T.zb[:, 0:16], T.S[:, 255:256], A.add, A.add)
+    al = S("sum", [sp, m], T.junk[:, 0:L], T.S[:, 0:L], 1.0, tb[:, 0:1], T.acl[:, 0:1])
+    y = V("ts", [sp, m], T.junk2[:, 0:L], T.S[:, 0:L], tb[:, 1:2], 0.0, A.add, A.is_lt)
+    if r == 1:
+        x = V("ts", [flg, kz], T.RB[:], T.zb[:, 0:32], T.fl[:, 0:1], None, A.add)
+        x = V("turn", [x], T.R16[:], T.RB[:])
+        k = V("tt", [k], T.tbe[:], T.De[:], T.Ke[:], A.subtract)
     if ex_out:
-        x = V("ts", [en, x], T.eI[:], T.bE[:], T.en[:, r:r + 1], None, A.subtract)
-        x = V("ts", [x], T.eJ[:], T.eI[:], 31, None, A.bitwise_and)
-        x = V("ts", [x], T.eT[:], T.eJ[:], T.S[:, 255:256], None, A.add)
-        x = V("ts", [x], T.eB[:], T.S[:, 256:272], T.eT[:], None, A.is_le)
-        x = V("red", [x], T.eR[:], T.eB[:])
-        V("ts", [x], T.iof[:, 10:11], T.eR[:], X0 + 240.0, None, A.add)
-    else: V("tt", [en], T.en[:, 4:6], T.en[:, 0:2], T.inf[:, 8:17:8], A.add)
-    x = V("ts", [al], T.cI[:], T.acl[:], -0.5, L / 2.0, A.mult, A.add)
-    V("ts", [], T.iof[:, 0:10:2], T.kk[:, 0:5], T.acl[:, 0:1], -0.5, A.add, A.mult)
-    x = V("ts", [x], T.jI[:], T.cI[:], 15, None, A.bitwise_and)
-    V("ts", [], T.iof[:, 1:10:2], T.kk[:, 0:5], T.acl[:, 1:2], -0.5, A.add, A.mult)
-    V("ts", [x], T.cf[:, 0:2], T.jI[:], 0.0, float(ZC), A.is_equal, A.mult)
-    x = V("ts", [], T.cf[:, 4:6], T.jI[:], 15.0, float(ZC), A.is_equal, A.mult)
-    io = V("tt", [x], T.iof[:, 0:6], T.iof[:, 0:6], T.cf[:], A.max)
+        k = V("scan", [x, k], T.Sl[:], T.R16[:, 0:16], T.zb[:, 0:16], 0.0, A.add, A.add)
+        ae = S("sum", [k], T.junk4[:], T.Sl[:], 4.0, T.tbe[:], T.ace[:])
+    y = V("scan", [y], T.junk3[:, 0:L], T.junk2[:, 0:L], T.zb[:, 0:L], -128.0, A.add, A.add)
+    x = V("ts", [y, kg], T.iof[:, 1:10:2], T.kv[:, 0:5], T.junk3[:, L - 1:L], None, A.add)
+    io = V("ts", [al], T.iof[:, 0:10:2], T.kk[:, 0:5], T.acl[:, 0:1], -0.5, A.add, A.mult)
 
     def nio(q): return 11 if r == 1 or (r == 0 and q < 2) else 10
+    def ncs(s, q): return ne if q == (1 if s == 0 else (s + 3) % N) else h2
     def block(t, k, q): return t[32 * k:32 * k + 32, 0:nio(q)]
     def spread(q, out): return [S("act", [io], block(out, k, q), block(T.iof, q, q), F.Copy) for k in range(4)][-1]
+    def more(): return V("ts", [ae], T.iof[:, 10:11], T.ace[:], -0.5, PB + 255.0 + 8, A.mult, A.add)
+    if r == 1: io = more()
     pls, pss = [], []
-    to = [(r + dq) % N for dq in range(1, N)]
+    to = [2, 3, 1] if r == 0 else [(r + dq) % N for dq in range(1, N)]
+    OF = [T["of%d" % at(q, r)][:, 0:nio(q)] for q in to]
+    SP = [T["sp%d" % at(q, r)] for q in to]
+    z = [V("copy", [io], block(T["of%d" % at(to[0], r)], k, to[0]), block(T.iof, to[0], to[0])) for k in range(4)][-1:]
+    if r == 0: io2 = more()
+    for n in (1, 2):
+        if r == 0 and n == 2: io = io2
+        z.append(spread(to[n], SP[n]))
     for n, q in enumerate(to):
-        i, j = at(q, r), at(r, q)
-        of, nq = T["of%d" % i], nio(q)
+        i, j, nq = at(q, r), at(r, q), nio(q)
         wd = 168 if nq == 11 else 160
-        if n == 0: y = [V("copy", [io], block(of, k, q), block(T.iof, q, q)) for k in range(4)][-1]
-        else: y = V("copy", [z], of[:, 0:nq], T["sp%d" % i][:, 0:nq])
-        z = spread(to[n + 1], T["sp%d" % at(to[n + 1], r)]) if n < 2 else None
-        off = of[:, 0:nq]
-        pq = V("copy", [y, hal, qz], U32(T["pkq%d" % i][:, 0:16 * nq]), U32(T.winq[:]).indirect(off))
-        pss.append(S("act", [y, hal, qz], T["pks%d" % i][:, 0:16 * nq], T.wins[:].indirect(off), F.Copy))
-        pls.append(([q], eng[q][4 * n:4 * n + 4], T.sem["cs%d" % j], T["pks%d" % i][:, 0:wd], [T.es[:, RG * r:RG * r + wd]]))
+        pq = V("copy", [z[n], pp, hal], U32(T["pkq%d" % i][:, 0:16 * nq]), U32(T.padq[:]).indirect(OF[n]))
+        if n == 0:
+            for o in (1, 2): z[o] = V("copy", [z[o]], OF[o], SP[o][:, 0:nio(to[o])])
+        pss.append(S("act", [z[n], pp, hal], T["pks%d" % i][:, 0:16 * nq], T.pads[:].indirect(OF[n]), F.Copy))
+        pls.append(([q], eng[q][n * h2:n * h2 + h2] if n < 2 else eng[q], T.sem["cs%d" % j], T["pks%d" % i][:, 0:wd], [T.es[:, RG * r:RG * r + wd]]))
+        if n == 2:
+            wait("p", pss[1:2])
+            send(pls[:2])
         wait("p", [pq])
         send([([q], eng[q], T.sem["cq%d" % j], U8(T["pkq%d" % i][:, 0:wd]), [U8(T.eq[:, RG * r:RG * r + wd])])])
-        if r == 0 and n == 1:
-            wait("p", pss[:1])
-            send(pls[:1])
     wait("p", pss[2:])
-    send(pls[1:] if r == 0 else pls)
-    x = V("tt", [en], T.en[:, 4:6], T.en[:, 0:2], T.inf[:, 8:17:8], A.add) if ex_out else None
+    send(pls[2:])
+
     z = spread(r, T.spo)
-    x = V("ts", [x], T.nen[:], T.en[:], -1.0, -0.5, A.mult, A.add)
+    en = V("scan", [own] + inf[:r] + inf[r + 1:], T.en[:, 0:4], T.inf[:, 0:32:8], T.zb[:, 0:4], -0.5 * U, A.add, A.add)
+    x = V("tt", [en, r0s], T.en[:, 4:6], T.en[:, 0:2], T.r0[:, 8:17:8], A.add)
     G = lambda c: T.g[:, 8 * c:8 * c + 8]
-    for c in (2, 3, 0, 1, 4, 5):
-        x = S("sign", [x], G(c), T.nP[:], T.nen[:, c:c + 1])
+    for n, c in ((4, 2), (5, 3), (0, 0), (2, 1), (1, 4), (3, 5)):
+        sg = S("sign", [x if c > 3 else en], G(n), T.nP[:], -1.0, T.en[:, c:c + 1])
+    ze = V("quant", [mz], T.eq[:, 4 * RG:4 * RG + 160], T.es[:, 4 * RG:4 * RG + 160], T.zt[:])
+    quant_w(0)
     no = nio(r)
     y = V("copy", [z], T.ioo[:, 0:no], T.spo[:, 0:no])
     off = T.ioo[:, 0:no]
-    pe = V("copy", [y], U32(T.eq[:, RG * r:RG * r + 16 * no]), U32(T.winq[:]).indirect(off))
-    pf = S("act", [y], T.es[:, RG * r:RG * r + 16 * no], T.wins[:].indirect(off), F.Copy)
-    y = V("tt", [x], T.gb[:], G(2), G(3), A.add)
-    V("tt", [], T.ga[:], G(0), G(1), A.add)
-    b = V("tt", [], T.gc1[:], G(4), G(5), A.add)
-    x = V("tt", [y], T.gs[:], T.gb[:], T.slot[:], A.add)
-    b = V("tt", [b], T.bb[:], T.ga[:], T.gc1[:], A.subtract) if r < 2 else V("tt", [], T.bb[:], G(1), G(5), A.subtract)
-    y = V("tt", [x], T.b0[:], T.ga[:], T.gs[:], A.add)
+    pe = V("copy", [y], U32(T.eq[:, RG * r:RG * r + 16 * no]), U32(T.padq[:]).indirect(off))
+    pf = S("act", [y], T.es[:, RG * r:RG * r + 16 * no], T.pads[:].indirect(off), F.Copy)
+    y = V("tt", [sg], T.gb[:], G(4), G(5), A.add)
+    b = V("tt", [], T.gac[:], T.g[:, 0:16], T.g[:, 16:32], A.add)
+    x = V("tt", [y], T.gs[:], T.slot[:], T.gb[:], A.subtract)
+    b = V("tt", [b], T.bb[:], T.gac[:, 0:8], T.gac[:, 8:16], A.subtract) if r < 2 else V("tt", [b], T.bb[:], G(2), G(3), A.subtract)
+    V("tt", [x], T.b1[:], T.gs[:], T.gac[:, 8:16], A.subtract)
     b = V("tt", [b], T.uu[:], T.bb[:], T.cE[:], A.mult)
-    x = V("tt", [], T.b1[:], T.gc1[:], T.gs[:], A.add)
-    V("ts", [y], T.fo[:], T.b0[:], RG / 2.0, None, A.mult)
-    b = V("tt", [b, x], T.b2[:], T.b1[:], T.uu[:], A.add)
-    fd = V("ts", [b], T.fu[:], T.b2[:], RG / 2.0, None, A.mult)
-    qw = V("quant", [ldw[2]], T.wq[:, W(2)], T.ws[:, W(2)], T.wt[:, W4(2)])
+    V("tt", [], T.bf[:, 0:8], T.gs[:], T.gac[:, 0:8], A.subtract)
+    b = V("tt", [b], T.bf[:, 8:16], T.b1[:], T.uu[:], A.subtract)
+    fd = V("ts", [b], T.fo[:], T.bf[:], RG / 2.0, None, A.mult)
+    quant_w(1)
 
-    cq = [("cq%d" % i, ne) for i in (2, 1, 0)]
-    cs = [("cs%d" % i, 4) for i in (2, 1, 0)]
-    for n, k in enumerate((0, 1, 2, 4, 3)):
+    cq = [("cq%d" % at(q, r), ne) for q in others]
+    cs = [("cs%d" % at(q, r), ncs(q, r)) for q in others]
+    for n, k in enumerate((1, 3, 4, 0, 2)):
         lo, hi = 128 * n, 128 * n + 128
         s = slice(32 * k, 32 * k + 4 * RG + 32)
-        off = (T.fu if k == 3 else T.fo)[:]
+        off = T.fo[:, 8:16] if k == 3 else T.fo[:, 0:8]
+        if n in (2, 3): quant_w(n)
         a = V("copy", [pe, fd] + cq, U32(T.xfq[:, lo:hi]), U32(T.eq[:, s]).indirect(off))
         b = S("act", [pf, fd, ze] + cs, T.xfs[:, lo:hi], T.es[:, s].indirect(off), F.Copy)
         ms = []
         for o in range(2):
-            w = 128 * (2 * KPOS[k] + o)
-            ms.append(op("t", "mm", [a, b, qw], T.yp[:, 512 * o:512 * o + 128], T.wq[:, w:w + 128], T.ws[:, w:w + 128],
-                         T.xfq[:, lo:hi], T.xfs[:, lo:hi], n == 0, n == 4))
+            w = 128 * (2 * n + o)
+            ms.append(op("t", "mm", [a, b, qw[n]], T.yp[:, 512 * o:512 * o + 128],
+                         T.wq[:, w:w + 128], T.ws[:, w:w + 128], T.xfq[:, lo:hi], T.xfs[:, lo:hi], n == 0, n == 4))
     x = V("copy", [ms[0]], T.ys[:, 0:128], T.yp[:, 0:128])
     dma("s", "st0", [x], T.y[:, 0:128], T.ys[:, 0:128])
     x = S("act", [ms[1]], T.ys[:, 128:256], T.yp[:, 512:640], F.Copy)
     dma("a", "st1", [x], T.y[:, 128:256], T.ys[:, 128:256])
     wait("p", [(k, n) for k, n in cnt.items()])
-    wait("p", [hal, inf, bdr, flg])
+    wait("p", [hal, bdr, flg, r0s] + inf[:r] + inf[r + 1:])

from concourse.bass import DstId, RemoteDMATransfer
from concourse.mybir import dt, AluOpType, ActivationFunctionType

A = AluOpType
F = ActivationFunctionType
CODE = "float8_e4m3fn_x4"
RG = 176
U = 1.0 / 128


def sb(n, d="float32"): return ("sbuf", [128, n], d)


BF, I32, U16 = "bfloat16", "int32", "uint16"
SCRATCH = {
    "ut": sb(512, BF), "xt": sb(1024, BF), "wt": sb(5120, BF), "zt": sb(640, BF), "xp": sb(1216, BF),
    "uq": sb(128, CODE), "us": sb(128, "uint8"), "urq": sb(128, CODE), "urs": sb(128, "uint8"),
    "xq": sb(256, CODE), "xs": sb(256, "uint8"), "padq": sb(544, CODE), "pads": sb(544, "uint8"),
    "wq": sb(1280, CODE), "ws": sb(1280, "uint8"),
    "eq": sb(4 * RG + 160, CODE), "es": sb(4 * RG + 160, "uint8"),
    "xfq": sb(640, CODE), "xfs": sb(640, "uint8"),
    "off0": sb(8, U16), "ys": sb(256),
    "sc": ("psum", [128, 1024], "float32"), "yp": ("psum", [128, 1024], "float32"),
    "pI": sb(1, I32), "pm": sb(4, I32), "pf": sb(4), "i64": sb(8), "i16": sb(8), "kk": sb(8), "kv": sb(8),
    "b2": sb(1), "b3": sb(1), "nb3": sb(1), "nb2": sb(1), "b7": sb(1), "p16": sb(1), "x8": sb(1),
    "tp": sb(2), "tp5": sb(2), "te": sb(1), "nP": sb(8), "slot": sb(8), "cE": sb(8), "half": sb(256, BF), "zb": sb(288, BF),
    "B": sb(64, BF), "BT": sb(64, BF), "EL": sb(64, BF), "eb": sb(64, BF),
    "P": sb(256, BF), "n2": sb(256, BF), "hp": sb(288, BF), "vp": sb(256, BF), "vn": sb(272, BF), "m1": sb(256, BF), "gh": sb(256, BF),
    "v2": sb(256, BF), "o2": sb(256, BF), "l": sb(256, BF), "S": sb(288, BF), "FT": sb(32, BF), "RB": sb(32, BF), "R16": sb(32, BF), "Sl": sb(16, BF),
    "bd": sb(16, BF), "inf": sb(32, BF), "r0": sb(32, BF), "fl": sb(8, BF),
    "D": sb(2), "D0": sb(2), "D5": sb(2), "K": sb(2, I32), "tb": sb(2), "E1": sb(1), "E5": sb(1), "De": sb(1), "Ke": sb(1, I32), "tbe": sb(1),
    "junk": sb(288, BF), "junk2": sb(288, BF), "junk3": sb(288, BF), "junk4": sb(16, BF), "acl": sb(2), "ace": sb(1), "iof": sb(12),
    "en": sb(6), "g": sb(48), "gac": sb(16), "gb": sb(8), "gs": sb(8), "b1": sb(8), "bb": sb(8), "uu": sb(8), "bf": sb(16),
    "fo": sb(16, U16), "ioo": sb(12, U16), "spo": sb(12),
}
for _i in range(3):
    SCRATCH["of%d" % _i] = sb(12, U16)
    SCRATCH["sp%d" % _i] = sb(12)
    SCRATCH["pkq%d" % _i] = sb(RG, CODE)
    SCRATCH["pks%d" % _i] = sb(RG, "uint8")
SEMAPHORES = ["vc", "ac", "tc", "pc", "ldu", "ldxa", "ldxb", "ldw0", "ldw1", "ldw2", "ldw3", "ldw4", "halo", "bdr", "inf0", "inf1", "inf2", "inf3",
              "r0s", "flg", "cq0", "cq1", "cq2", "cs0", "cs1", "cs2", "sent", "st0", "st1"]


def rank_program(g, core, T, topo):
    r = T.rank_of(core)
    if r is None:
        return
    N = len(T.cores)
    others = [q for q in range(N) if q != r]
    Q = {"v": g.vector, "a": g.scalar, "t": g.tensor, "p": g, "s": g.sync}
    cnt, seen = {"sent": 0}, {}

    def wait(qn, deps):
        for d in deps:
            if d is not None and seen.get((qn, d[0]), 0) < d[1]:
                Q[qn].wait_ge(T.sem[d[0]], d[1])
                seen[(qn, d[0])] = d[1]

    def tok(sem, inst, n):
        inst.then_inc(T.sem[sem], n)
        cnt[sem] = cnt.get(sem, 0) + n
        return (sem, cnt[sem])

    def op(qn, name, deps, *args):
        wait(qn, deps)
        q = Q[qn]
        if name == "memset": i = q.memset(*args)
        elif name == "tt": i = q.tensor_tensor(*args)
        elif name == "ts": i = q.tensor_scalar(*args)
        elif name == "copy": i = q.tensor_copy(*args)
        elif name == "scan": i = q.tensor_tensor_scan(*args)
        elif name == "turn": i = q.transpose(*args)
        elif name == "quant": i = q.quantize_mx(*args)
        elif name == "act": i = q.activation(*args)
        elif name == "lin": i = q.activation(args[0], args[1], F.Identity, bias=args[3], scale=args[2])
        elif name == "sign": i = q.activation(args[0], args[1], F.Sign, bias=args[3], scale=args[2])
        elif name == "sum": i = q.activation(args[0], args[1], F.Sign, bias=args[3], scale=args[2], accum_out=args[4])
        elif name == "mm": i = q.matmul_mx(*args)
        elif name == "iota": i = q.iota(*args)
        else: i = q.iota(*args, allow_small_or_imprecise_dtypes=True)
        return tok(qn + "c", i, 1)

    def V(name, deps, *args): return op("v", name, deps, *args)
    def S(name, deps, *args): return op("a", name, deps, *args)

    def dma(qn, sem, deps, out, in_):
        wait(qn, deps)
        return tok(sem, Q[qn].dma_start(out, in_), 16)

    def U8(v): return v.bitcast(dt.uint8)
    def U32(v): return v.bitcast(dt.uint32)
    def bits(en): return sum(1 << e for e in en)

    def dest(q):
        rid, pid, _ = topo.addr(T.cores[q])
        return DstId(rid=rid, pnc=pid)

    def send(trs):
        g.remote_dma_fused([RemoteDMATransfer(dst_ids=[dest(q) for q in qs], dma_engine_mask=bits(en), remote_sem=sem, srcs=[src], dsts=dsts)
                            for qs, en, sem, src, dsts in trs], local_sem=T.sem.sent)
        cnt["sent"] += sum(len(t[1]) for t in trs)

    def at(q, me): return q if q < me else q - 1
    eng = {q: topo.engines(core, T.cores[q]) for q in others}
    ne = min(len(eng[q]) for q in others)
    e0 = eng[others[0]]
    h2 = ne // 2

    up, dn = r > 0, r < N - 1
    ex_out, ex_in = r in (0, 1), r in (1, 2)
    PB = 128 if dn else 129
    L = 288 if r == 0 else 272
    ldu = dma("a", "ldu", [], T.ut[:, 0:8], T.u[:, 0:8])
    h0, h1 = (0, 1) if up else (1, 0)
    X = lambda h: slice(512 * h, 512 * h + 512)
    ldxa = dma("s", "ldxa", [], T.xt[:, X(h0)], T.x[:, X(h0)])
    ldxb = dma("a", "ldxb", [], T.xt[:, X(h1)], T.x[:, X(h1)])
    kp = op("p", "iota", [], T.pI[:], [[0, 1]], 0, 1)
    op("p", "iotaf", [], T.i64[:], [[64, 8]], 0, 0)
    op("p", "iotaf", [], T.i16[:], [[0, 4], [16, 2]], 0, 0)
    op("p", "iotaf", [], T.kk[:, 0:3], [[-2, 3]], -2 * (PB - 1) - L, 0)
    op("p", "iotaf", [], T.kk[:, 3:5], [[-68, 2]], -2 * (PB - 17) - L, 0)
    op("p", "iotaf", [], T.kv[:, 0:3], [[1, 3]], PB - 1 + 128, 0)
    kg = op("p", "iotaf", [], T.kv[:, 3:5], [[34, 2]], PB - 17 + 128, 0)
    mu = V("memset", [], T.ut[:, 8:512], 0.0)
    mo = V("memset", [], T.off0[:], 0)
    V("ts", [kp], T.pm[:, 3:4], T.pI[:], 5, None, A.logical_shift_right)
    V("ts", [], T.pm[:, 0:1], T.pI[:], 15, None, A.bitwise_and)
    V("ts", [], T.pm[:, 1:2], T.pI[:], 7, None, A.bitwise_and)
    k = V("ts", [], T.pm[:, 2:3], T.pI[:], 3, 1, A.logical_shift_right, A.bitwise_and)
    mB = V("memset", [], T.B[:], 0.0)
    kf = V("copy", [k], T.pf[:], T.pm[:])
    mz = V("memset", [], T.zt[:], 0.0)

    qu = V("quant", [ldu, mu], T.uq[:], T.us[:], T.ut[:])
    pu = V("copy", [qu, mo], U32(T.urq[:]), U32(T.uq[:]).indirect(T.off0[:]))
    pv = S("act", [qu, mo], T.urs[:], T.us[:].indirect(T.off0[:]), F.Copy)
    qx, mm = {}, {}

    def score(h, ld):
        c = slice(128 * h, 128 * h + 128)
        qx[h] = V("quant", [ld], T.xq[:, c], T.xs[:, c], T.xt[:, X(h)])
        mm[h] = op("t", "mm", [pu, pv, qx[h]], T.sc[:, 512 * h:512 * h + 128], T.urq[:], T.urs[:], T.xq[:, c], T.xs[:, c], True, True)
    score(h0, ldxa)
    V("memset", [], T.half[:], 0.5)
    V("memset", [], T.vn[:, 0:16], -3.0)
    V("memset", [], T.vn[:, 256:272], -3.0)
    kz = V("memset", [], T.zb[:], 0.0)
    score(h1, ldxb)
    ldw, qw = {}, {}

    def load_w(k, deps): ldw[k] = dma("s", "ldw%d" % k, deps, T.wt[:, 1024 * k:1024 * k + 1024], T.w[:, 1024 * k:1024 * k + 1024])
    def quant_w(k): qw[k] = V("quant", [ldw[k]], T.wq[:, 256 * k:256 * k + 256], T.ws[:, 256 * k:256 * k + 256], T.wt[:, 1024 * k:1024 * k + 1024])
    load_w(4, [ldxb])

    nb = ([(r - 1, 0, 400)] if up else []) + ([(r + 1, 240, 112)] if r == N - 2 else [])

    def strips(view, nb):
        if nb:
            send([([q], eng[q][(src > 0) * h2:(src > 0) * h2 + h2], T.sem.halo, view("xq", "xs", src), [view("padq", "pads", dst)]) for q, src, dst in nb])
    for b in nb:
        wait("p", [qx[b[1] > 0]])
        strips(lambda q, s, a: U8(T[q][:, a:a + 16]), [b])
    hal = ("halo", 2 * h2)

    S("lin", [kf, kg], T.b2[:], T.pf[:, 2:3], 32.0, T.pf[:, 1:2])
    k = S("lin", [], T.p16[:], T.pf[:, 0:1], 2.0 / RG, 4 + 0.5 / RG)
    k = S("lin", [k], T.b3[:], T.pf[:, 3:4], 8.0, T.b2[:])
    k = S("lin", [k], T.nb3[:], T.b3[:], -U, -0.5 * U)
    S("lin", [], T.x8[:], T.pf[:, 2:3], -8.0 / RG, 64.0 / RG)
    k = S("lin", [k], T.tp[:], T.i64[:, 0:2], -U, T.nb3[:])
    S("lin", [], T.b7[:], T.pf[:, 3:4], 8.0, T.pf[:, 1:2])
    k = S("lin", [k], T.tp5[:], T.tp[:], 1.0, 0.5)
    S("lin", [], T.nb2[:], T.b2[:], U, 8.0 * r * U)
    S("lin", [k], T.te[:], T.b7[:], -1.0 / 32, -0.5 / 32)
    k = S("lin", [], T.slot[:], T.i16[:], 2.0 / RG, T.p16[:])
    S("lin", [k], T.nP[:], T.i64[:], U, T.nb2[:])
    kS = S("lin", [], T.cE[:], T.i16[:], -1.0 / RG, T.x8[:])
    xp0 = 128 if dn else 4
    for i in range(16): kX = S("act", [ldxa, ldxb], T.xp[:, xp0 + 68 * i:xp0 + 68 * i + 64], T.xt[:, 64 * i:64 * i + 64], F.Copy)

    if up: kb = V("ts", [mm[0], mB], T.B[:, 32:48], T.sc[:, 0:16], 0.0, None, A.is_gt)
    if dn: kb = V("ts", [mm[1], mB], T.B[:, 0:16], T.sc[:, 624:640], 0.0, None, A.is_gt)
    kb = V("turn", [kb], T.BT[:], T.B[:])
    for h in (h0, h1): p = V("ts", [mm[h]], T.P[:, 128 * h:128 * h + 128], T.sc[:, 512 * h:512 * h + 128], 0.0, None, A.is_gt)
    wait("p", [kb])
    send(([([r - 1], eng[r - 1][:h2], T.sem.bdr, T.BT[:, 32:33], [T.bd[:, 8:9]])] if up else [])
         + ([([r + 1], eng[r + 1][h2:], T.sem.bdr, T.BT[:, 0:1], [T.bd[:, 0:1]])] if dn else []))
    strips(lambda q, s, a: T[s][:, a:a + 16], nb)
    n2 = V("ts", [p], T.n2[:], T.P[:], -2.0, None, A.add)
    h = V("scan", [n2, kz], T.hp[:, 16:271], T.P[:, 0:255], T.n2[:, 1:256], -100.0, A.max, A.add)
    v = V("scan", [], T.vp[:, 0:240], T.P[:, 0:240], T.n2[:, 16:256], -100.0, A.max, A.add)
    h = V("memset", [h], T.hp[:, 31:272:16], 0.0)
    v = V("ts", [v], T.vn[:, 16:256], T.vp[:, 0:240], -1.0, -3.0, A.is_equal, A.add)
    h = V("ts", [h], T.m1[:], T.hp[:, 16:272], -1.0, None, A.is_equal)
    v = V("scan", [v], T.v2[:], T.vn[:, 16:272], T.vn[:, 0:256], -100.0, A.max, A.add)
    h = V("scan", [h], T.gh[:], T.half[:], T.m1[:], 0.0, A.mult, A.max)
    V("memset", [], T.xp[:, 0:128] if dn else T.xp[:, 1088:1216], 0.0)
    h = V("scan", [h, v], T.o2[:], T.gh[:], T.v2[:], -100.0, A.max, A.add)
    load_w(0, [h])
    l = V("ts", [h], T.l[:], T.o2[:], -5.6, U, A.is_gt, A.mult)
    for t in range(4): mp = V("memset", [], T.xp[:, (192 if dn else 0) + t:1216 if dn else 1088:68], 0.0)

    bdr = ("bdr", h2 * len([q for q in (r - 1, r + 1) if 0 <= q < N]))
    a, b = (0 if up else 32), (64 if dn else 32)
    if up: x = V("ts", [bdr], T.EL[:, 0:32], T.BT[:, 32:64], T.bd[:, 0:1], U, A.not_equal, A.mult)
    if dn: x = V("ts", [bdr], T.EL[:, 32:64], T.BT[:, 0:32], T.bd[:, 8:9], U, A.not_equal, A.mult)
    x = V("turn", [x], T.eb[:, a:b], T.EL[:, a:b])
    if up: l = V("tt", [x, l], T.l[:, 0:16], T.l[:, 0:16], T.eb[:, 0:16], A.max)
    if dn: l = V("tt", [x, l], T.l[:, 240:256], T.l[:, 240:256], T.eb[:, 32:48], A.max)
    sS = V("scan", [l], T.S[:, 0:256], T.l[:], T.zb[:, 0:256], 0.0, A.add, A.add)
    if ex_in: ft = V("turn", [], T.FT[:], T.l[:, 0:32])
    wait("p", [sS])
    down = others[::-1]
    send([(down, e0, T.sem["inf%d" % r], T.S[:, 255:256], [T.inf[:, 8 * r:8 * r + 1]] * 3)])
    if ex_in:
        wait("p", [ft])
        send([([r - 1], e0[h2:], T.sem.flg, T.FT[:, 0:1], [T.fl[:, 0:1]]),
              (down, e0[:h2], T.sem.r0s, T.S[:, 15:16], [T.r0[:, 8 * r:8 * r + 1]] * 3)])
    inf = [("inf%d" % q, ne) for q in range(N)]
    r0s = ("r0s", h2 * (1 if ex_in else 2))
    flg = ("flg", h2) if ex_out else None

    sp = V("copy", [sS], T.S[:, 256:272], T.S[:, 15:256:16])
    own = V("copy", [], T.inf[:, 8 * r:8 * r + 1], T.S[:, 255:256])
    if ex_in: own = V("copy", [], T.r0[:, 8 * r:8 * r + 1], T.S[:, 15:16])
    if ex_out: E1 = V("ts", [kS], T.E1[:], T.S[:, 255:256], 4.0, T.te[:], A.mult, A.add)
    if dn: V("quant", [mz], T.padq[:, 416:544], T.pads[:, 416:544], T.zt[:, 0:512])
    if ex_out: V("ts", [E1], T.E5[:], T.E1[:], 0.5, None, A.add)
    a = 96 if dn else 128
    pp = V("quant", [kX, mp], T.padq[:, a:a + 304], T.pads[:, a:a + 304], T.xp[:])
    for k in (1, 2, 3): load_w(k, [pp])
    quant_w(4)

    if r == 0: tb, m = T.tp, kS
    else:
        tb = T.tb
        i0, i1, i2 = T.inf[:, 0:1], T.inf[:, 8:9], T.inf[:, 16:17]
        if r == 1:
            V("ts", [kS, inf[0]], T.D[:], T.tp[:], i0, None, A.add)
            x = V("ts", [], T.K[:], T.tp5[:], i0, None, A.add)
            V("ts", [], T.De[:], i0, 4.0, T.E1[:], A.mult, A.add)
        else:
            a, b = (T.D, T.K) if r == 2 else (T.D0, T.D5)
            V("ts", [kS, inf[0], inf[1]], a[:], T.tp[:], i0, i1, A.add, A.add)
            x = V("ts", [], b[:], T.tp5[:], i0, i1, A.add, A.add)
            if r == 3:
                V("ts", [x, inf[2]], T.D[:], T.D0[:], i2, None, A.add)
                x = V("ts", [], T.K[:], T.D5[:], i2, None, A.add)
        m = V("tt", [x], T.tb[:], T.D[:], T.K[:], A.subtract)
        if r == 1: k = V("ts", [], T.Ke[:], i0, 4.0, T.E5[:], A.mult, A.add)
    if r == 0:
        k = V("ts", [], T.Ke[:], T.E1[:], 0.5, None, A.add)
        x = V("ts", [flg, kz], T.RB[:], T.zb[:, 0:32], T.fl[:, 0:1], None, A.add)
        k = V("tt", [k], T.tbe[:], T.E1[:], T.Ke[:], A.subtract)
        x = V("turn", [x], T.R16[:], T.RB[:])
        sp = V("scan", [x], T.S[:, 272:288], T.R16[:, 0:16], T.zb[:, 0:16], T.S[:, 255:256], A.add, A.add)
    al = S("sum", [sp, m], T.junk[:, 0:L], T.S[:, 0:L], 1.0, tb[:, 0:1], T.acl[:, 0:1])
    y = V("ts", [sp, m], T.junk2[:, 0:L], T.S[:, 0:L], tb[:, 1:2], 0.0, A.add, A.is_lt)
    if r == 1:
        x = V("ts", [flg, kz], T.RB[:], T.zb[:, 0:32], T.fl[:, 0:1], None, A.add)
        x = V("turn", [x], T.R16[:], T.RB[:])
        k = V("tt", [k], T.tbe[:], T.De[:], T.Ke[:], A.subtract)
    if ex_out:
        k = V("scan", [x, k], T.Sl[:], T.R16[:, 0:16], T.zb[:, 0:16], 0.0, A.add, A.add)
        ae = S("sum", [k], T.junk4[:], T.Sl[:], 4.0, T.tbe[:], T.ace[:])
    y = V("scan", [y], T.junk3[:, 0:L], T.junk2[:, 0:L], T.zb[:, 0:L], -128.0, A.add, A.add)
    x = V("ts", [y, kg], T.iof[:, 1:10:2], T.kv[:, 0:5], T.junk3[:, L - 1:L], None, A.add)
    io = V("ts", [al], T.iof[:, 0:10:2], T.kk[:, 0:5], T.acl[:, 0:1], -0.5, A.add, A.mult)

    def nio(q): return 11 if r == 1 or (r == 0 and q < 2) else 10
    def ncs(s, q): return ne if q == (1 if s == 0 else (s + 3) % N) else h2
    def block(t, k, q): return t[32 * k:32 * k + 32, 0:nio(q)]
    def spread(q, out): return [S("act", [io], block(out, k, q), block(T.iof, q, q), F.Copy) for k in range(4)][-1]
    def more(): return V("ts", [ae], T.iof[:, 10:11], T.ace[:], -0.5, PB + 255.0 + 8, A.mult, A.add)
    if r == 1: io = more()
    pls, pss = [], []
    to = [2, 3, 1] if r == 0 else [(r + dq) % N for dq in range(1, N)]
    OF = [T["of%d" % at(q, r)][:, 0:nio(q)] for q in to]
    SP = [T["sp%d" % at(q, r)] for q in to]
    z = [V("copy", [io], block(T["of%d" % at(to[0], r)], k, to[0]), block(T.iof, to[0], to[0])) for k in range(4)][-1:]
    if r == 0: io2 = more()
    for n in (1, 2):
        if r == 0 and n == 2: io = io2
        z.append(spread(to[n], SP[n]))
    for n, q in enumerate(to):
        i, j, nq = at(q, r), at(r, q), nio(q)
        wd = 168 if nq == 11 else 160
        pq = V("copy", [z[n], pp, hal], U32(T["pkq%d" % i][:, 0:16 * nq]), U32(T.padq[:]).indirect(OF[n]))
        if n == 0:
            for o in (1, 2): z[o] = V("copy", [z[o]], OF[o], SP[o][:, 0:nio(to[o])])
        pss.append(S("act", [z[n], pp, hal], T["pks%d" % i][:, 0:16 * nq], T.pads[:].indirect(OF[n]), F.Copy))
        pls.append(([q], eng[q][n * h2:n * h2 + h2] if n < 2 else eng[q], T.sem["cs%d" % j], T["pks%d" % i][:, 0:wd], [T.es[:, RG * r:RG * r + wd]]))
        if n == 2:
            wait("p", pss[1:2])
            send(pls[:2])
        wait("p", [pq])
        send([([q], eng[q], T.sem["cq%d" % j], U8(T["pkq%d" % i][:, 0:wd]), [U8(T.eq[:, RG * r:RG * r + wd])])])
    wait("p", pss[2:])
    send(pls[2:])

    z = spread(r, T.spo)
    en = V("scan", [own] + inf[:r] + inf[r + 1:], T.en[:, 0:4], T.inf[:, 0:32:8], T.zb[:, 0:4], -0.5 * U, A.add, A.add)
    x = V("tt", [en, r0s], T.en[:, 4:6], T.en[:, 0:2], T.r0[:, 8:17:8], A.add)
    G = lambda c: T.g[:, 8 * c:8 * c + 8]
    for n, c in ((4, 2), (5, 3), (0, 0), (2, 1), (1, 4), (3, 5)):
        sg = S("sign", [x if c > 3 else en], G(n), T.nP[:], -1.0, T.en[:, c:c + 1])
    ze = V("quant", [mz], T.eq[:, 4 * RG:4 * RG + 160], T.es[:, 4 * RG:4 * RG + 160], T.zt[:])
    quant_w(0)
    no = nio(r)
    y = V("copy", [z], T.ioo[:, 0:no], T.spo[:, 0:no])
    off = T.ioo[:, 0:no]
    pe = V("copy", [y], U32(T.eq[:, RG * r:RG * r + 16 * no]), U32(T.padq[:]).indirect(off))
    pf = S("act", [y], T.es[:, RG * r:RG * r + 16 * no], T.pads[:].indirect(off), F.Copy)
    y = V("tt", [sg], T.gb[:], G(4), G(5), A.add)
    b = V("tt", [], T.gac[:], T.g[:, 0:16], T.g[:, 16:32], A.add)
    x = V("tt", [y], T.gs[:], T.slot[:], T.gb[:], A.subtract)
    b = V("tt", [b], T.bb[:], T.gac[:, 0:8], T.gac[:, 8:16], A.subtract) if r < 2 else V("tt", [b], T.bb[:], G(2), G(3), A.subtract)
    V("tt", [x], T.b1[:], T.gs[:], T.gac[:, 8:16], A.subtract)
    b = V("tt", [b], T.uu[:], T.bb[:], T.cE[:], A.mult)
    V("tt", [], T.bf[:, 0:8], T.gs[:], T.gac[:, 0:8], A.subtract)
    b = V("tt", [b], T.bf[:, 8:16], T.b1[:], T.uu[:], A.subtract)
    fd = V("ts", [b], T.fo[:], T.bf[:], RG / 2.0, None, A.mult)
    quant_w(1)

    cq = [("cq%d" % at(q, r), ne) for q in others]
    cs = [("cs%d" % at(q, r), ncs(q, r)) for q in others]
    for n, k in enumerate((1, 3, 4, 0, 2)):
        lo, hi = 128 * n, 128 * n + 128
        s = slice(32 * k, 32 * k + 4 * RG + 32)
        off = T.fo[:, 8:16] if k == 3 else T.fo[:, 0:8]
        if n in (2, 3): quant_w(n)
        a = V("copy", [pe, fd] + cq, U32(T.xfq[:, lo:hi]), U32(T.eq[:, s]).indirect(off))
        b = S("act", [pf, fd, ze] + cs, T.xfs[:, lo:hi], T.es[:, s].indirect(off), F.Copy)
        ms = []
        for o in range(2):
            w = 128 * (2 * n + o)
            ms.append(op("t", "mm", [a, b, qw[n]], T.yp[:, 512 * o:512 * o + 128],
                         T.wq[:, w:w + 128], T.ws[:, w:w + 128], T.xfq[:, lo:hi], T.xfs[:, lo:hi], n == 0, n == 4))
    x = V("copy", [ms[0]], T.ys[:, 0:128], T.yp[:, 0:128])
    dma("s", "st0", [x], T.y[:, 0:128], T.ys[:, 0:128])
    x = S("act", [ms[1]], T.ys[:, 128:256], T.yp[:, 512:640], F.Copy)
    dma("a", "st1", [x], T.y[:, 128:256], T.ys[:, 128:256])
    wait("p", [(k, n) for k, n in cnt.items()])
    wait("p", [hal, bdr, flg, r0s] + inf[:r] + inf[r + 1:])
